import numpy as np, ml_dtypes
CORES = [2,3,42,43,82,83,122,123]
N = 8
BF = ml_dtypes.bfloat16
def gentries(a):
    return np.ascontiguousarray(a.reshape(8, 16, -1).transpose(0, 2, 1)).reshape(8, -1)
def gtable(e):
    e = np.asarray(e); return np.ascontiguousarray(e.reshape(8, -1, 16).transpose(0, 2, 1)).reshape(128, -1).astype(np.int32)
V, W, SH, CH, RO = 512, 8192, 1, 2, 3
def parts(rng):
    s = rng.integers(0, 256, (N, 8, 16, W), dtype=np.uint8); x = rng.integers(0, 256, (N, 8, 16, V), dtype=np.uint8)
    r = rng.integers(0, 256, (N, 8, 16, V)); r = np.where(rng.random((N, 8, 1, V)) < 0.5, r, 64 + (r >> 1))
    nx = rng.integers(0, V, (N, 8, V)); sr = rng.integers(0, V, (N, 8, V)); ft = rng.integers(17000, 27000, (N, 8, V))
    return s, r, x, nx, sr, ft
def pack(s, r, x, nx, sr, ft):
    return {"prof": s.reshape(N, 128, W).astype(np.float32).astype(BF), "resid": np.ascontiguousarray(r.reshape(N, 128, V)).astype(np.int32), "obs": x.reshape(N, 128, V).astype(np.float32).astype(BF),
            "nx0": np.stack([gtable(a) for a in nx]), "src0": np.stack([gtable(a) for a in sr]), "fit0": np.ascontiguousarray(ft.reshape(N, 8, V)).astype(np.int32)}
def setup_inputs(rng):
    return pack(*parts(rng))
def setup_inputs_spread(rng):
    s = np.minimum(np.exp2(8 * rng.random((N, 8, 1, W))) * rng.random((N, 8, 16, W), dtype=np.float32), 255).astype(np.uint8)
    x = np.minimum(np.exp2(8 * rng.random((N, 8, 1, V))) * rng.random((N, 8, 16, V)), 255).astype(np.uint8)
    r = np.minimum(np.exp2(8 * rng.random((1, 8, 16, 1))) * rng.random((N, 8, 16, V)), 255).astype(np.int64)
    nx = np.minimum((V * rng.random((N, 8, V)) ** 3).astype(np.int64), V - 1); sr = V - 1 - np.minimum((V * rng.random((N, 8, V)) ** 3).astype(np.int64), V - 1)
    ft = np.minimum(np.exp2(16 * rng.random((N, 8, V)) ** 0.5), 65535).astype(np.int64)
    return pack(s, r, x, nx, sr, ft)
def setup_inputs_ends(rng):
    s, r, x, nx, sr, ft = parts(rng)
    s = 255 * rng.integers(0, 2, (N, 8, 16, W), dtype=np.uint8); x = 255 * rng.integers(0, 2, (N, 8, 16, V), dtype=np.uint8)
    cnt = np.clip(np.array([8, 16, 8, 0, 8, 16, 8, 8])[None, :, None] + rng.integers(-1, 2, (N, 8, V)), 0, 16)
    r = np.where(np.argsort(rng.random((N, 8, 16, V)), axis=2) < cnt[:, :, None, :], 255, 0)
    alt = 255 * (np.arange(16) & 1); r[:, 7, :, 0] = alt; r[:, 7, :, V - 1] = 255 - alt; r[N - 1, 7, 15, V - 1] = 255
    for q in range(N):
        for g in range(8):
            if (N - 1 - q + 7 - g) % 2 == 0:
                bit = rng.permutation(np.array([0, 1] + [int(b) for b in rng.integers(0, 2, 14)])).astype(np.uint8); row = (255 * bit)[:, None]
                s[q, g] = row; kind = rng.integers(0, 4, V); kind[0] = 0; kind[V - 1] = 0
                x[q, g] = np.where(kind[None, :] < 2, 255 - row, np.where(kind[None, :] == 2, row, x[q, g]))
    ft = np.where(rng.random((N, 8, V)) < 0.7, 65535, 0); ft[:, :, 0] = 65535; ft[:, :, V - 1] = 65535
    nx = np.where(rng.random((N, 8, V)) < 0.8, (V - 1) * rng.integers(0, 2, (N, 8, V)), nx); sr = np.where(rng.random((N, 8, V)) < 0.8, (V - 1) * rng.integers(0, 2, (N, 8, V)), sr)
    nx[:, :, V - 1] = V - 1; sr[:, :, V - 1] = 0
    return pack(s, r, x, nx, sr, ft)
def setup_inputs_corners(rng):
    s, r, x, nx, sr, ft = parts(rng); own = np.arange(V)
    for q in range(N):
        r[q, 0:2] = rng.integers(0, 8, (2, 16, V)) if q % 2 == 0 else rng.integers(248, 256, (2, 16, V))
    v = rng.integers(0, 2, (N, 2, 8, V)); e = 128 + np.concatenate([v, -v], axis=2)
    e = np.take_along_axis(e, np.argsort(rng.random(e.shape), axis=2), 2)
    d = np.where((own & 1) == 1, rng.choice(np.array([-129, -128, -127, -1, 0, 1, 126, 127, 128]), (N, 2, V)), 0)
    e[:, :, 0] += d >> 1; e[:, :, 15] += d - (d >> 1); r[:, 2:4] = e
    nx[:, 2:4] = 2 * rng.integers(0, V // 2, (N, 2, V)); sr[:, 2:4] = 2 * rng.integers(0, V // 2, (N, 2, V))
    top = rng.random((N, 1, V)) < 0.5; low = np.zeros((N, 16, V), np.int64)
    np.put_along_axis(low, rng.integers(0, 16, (N, 1, V)), rng.choice(np.array([0, 0, 1, 2, 100, 254, 255]), (N, 1, V)), 1)
    r[:, 4] = np.where(top, 255 - low, low)
    for q in range(N):
        for g in range(8):
            m = (q + g) % 6
            if g not in (2, 3):
                if m == 0: nx[q, g] = own; sr[q, g] = own
                if m == 1: nx[q, g] = 0; sr[q, g] = V - 1
                if m == 2: nx[q, g] = V - 1; sr[q, g] = 0
                if m == 3: nx[q, g] = own; sr[q, g] = (own + 1) % V
                if m == 4: nx[q, g] = np.stack([0 * own, 0 * own + V - 1, own])[rng.integers(0, 3, V), own]
            m = (2 * q + g) % 5
            if m == 0: ft[q, g] = 0
            if m == 1: ft[q, g] = 65535
            if m == 2: ft[q, g] = rng.choice(np.array([0, 1, 7, 8, 20000, 65279, 65280, 65281, 65535]), V)
    return pack(s, r, x, nx, sr, ft)
def setup_inputs_near(rng):
    s, r, x, nx, sr, ft = parts(rng); own = np.arange(V)
    mid = 112 + (r[:, 5:7] & 15); s = s & 3; x = x & 3; r[:, ::2] = r[:, ::2] & 3; r[:, 5:7] = mid
    sr = np.where(rng.random((N, 8, V)) < 0.25, own, sr); ft = rng.integers(285, 336, (N, 8, V))
    ft[:, 5:7] = np.where(rng.random((N, 2, V)) < 0.5, 65535, ft[:, 5:7])
    return pack(s, r, x, nx, sr, ft)
def setup_inputs_rounds(rng):
    s, r, x, nx, sr, ft = parts(rng); m = V - N; e = np.arange(m); st = (3 * e) // m
    for g in range(8):
        if g in (3, 7):
            s[:, g] = s[:, g] & 3; x[:, g] = x[:, g] & 3; r[:, g] = 112 + (r[:, g] & 7); ft[:, g] = 65535
            continue
        o = rng.permutation(V); tg = o[:N]
        for q in range(N):
            row = 255 * rng.integers(0, 2, (16, 1)); kind = rng.integers(0, 3, (1, V))
            d = np.where(kind == 0, 255, np.where(kind == 1, 255 - rng.integers(0, 101, (16, V)), rng.integers(0, 128, (16, V))))
            s[q, g] = row.astype(np.uint8); x[q, g] = np.where(row == 0, d, 255 - d).astype(np.uint8)
            mid = 112 + (r[q, g] & 7); mid[:, tg[np.arange(N) != q]] = rng.integers(0, 8, (16, N - 1)) + 248 * rng.integers(0, 2, (1, N - 1)); r[q, g] = mid
            sl = rng.permutation(o[N:]); nx[q, g, tg] = tg; sr[q, g, tg] = tg; nx[q, g, sl] = tg[(q + 1 + st) % N]
            w = 1 + (q + 3 * g) % 7; c = 8 * int(rng.integers(1, 4)) + w
            later = e % (w + 1) if (q + g) % 2 == 0 else e % 10
            off = np.where(st == 0, np.where(e < c, 1 + e % 9, -(e % 9)), np.where(st == 1, later, e % 10))
            ft[q, g] = 0; ft[q, g, sl] = np.maximum(16 * np.add.reduce(d, axis=0)[sl] + off, 0)
    return pack(s, r, x, nx, sr, ft)
def check_inputs(d):
    bad = []
    for k, lo, hi in (("prof", 0, 255), ("resid", 0, 255), ("obs", 0, 255), ("nx0", 0, V - 1), ("src0", 0, V - 1), ("fit0", 0, 65535)):
        v = np.asarray(d[k]).astype(np.float64)
        if not (np.min(v) >= lo and np.max(v) <= hi): bad.append("range of " + k)
        elif np.any(v != np.floor(v)): bad.append("whole numbers of " + k)
    return bad
def reference(prof, resid, obs, nx0, src0, fit0):
    sp = np.ascontiguousarray(prof.astype(np.float32).astype(np.int16).reshape(N, 8, 16, W).transpose(0, 1, 3, 2)).reshape(N, 8 * W, 16)
    ob = np.ascontiguousarray(obs.astype(np.float32).astype(np.int16).reshape(N, 8, 16, V).transpose(0, 1, 3, 2))
    r = resid.astype(np.int64).reshape(N, 8, 16, V); ft = fit0.astype(np.int64)
    nx = np.stack([gentries(a) for a in nx0]).astype(np.int64); sr = np.stack([gentries(a) for a in src0]).astype(np.int64)
    acc = np.zeros((N, 8), np.int64); odd = 2 * np.arange(V) + 1; first = (np.arange(8) * W)[:, None, None]; site = np.arange(16)[None, :, None]; none = 2 ** 20
    def cost(a, p):
        col = ((odd * (p + 4096)) >> SH) & (W - 1)
        return np.add.reduce(np.abs(np.take(sp[a], first + col, axis=0) - ob[a][:, None]), axis=-1, dtype=np.int64)
    for t in range(RO):
        tot = np.add.reduce(r, axis=2); r2, nx2, sr2, ft2, took = [], [], [], [], []
        for a in range(N):
            q = (a + 1 + t % (N - 1)) % N; n = nx[a]
            best = np.full((8, V), none, np.int64); bn = np.zeros((8, V), np.int64); bl = r[a]
            for z in range(CH):
                if z > 0: n = np.take_along_axis(sr[q], n, 1)
                l = np.take_along_axis(r[q], n[:, None, :], 2)
                dl = (tot[a] - np.take_along_axis(tot[q], n, 1))[:, None, :]
                p = np.add.accumulate(l, axis=1); g = cost(a, p); h = cost(a, p + dl)
                sc = np.add.accumulate(g, axis=1) - g + np.add.accumulate(h[:, ::-1], axis=1)[:, ::-1]
                sc = np.where((l + dl >= 0) & (l + dl <= 255), sc, none)
                j = np.argmin(sc, axis=1); m = np.min(sc, axis=1); better = m < best
                bl = np.where(better[:, None, :], l + np.where(site == j[:, None, :], dl, 0), bl)
                bn = np.where(better, n, bn); best = np.where(better, m, best)
            ok = best < ft[a] - (acc[a] & 7)[:, None]
            r2.append(np.where(ok[:, None, :], bl, r[a])); ft2.append(np.where(ok, best, ft[a])); sr2.append(np.where(ok, bn, sr[a]))
            nx2.append(np.where(ok, (13 * bn + best) & (V - 1), n)); took.append(np.add.reduce(ok.astype(np.int64), axis=1))
        r, nx, sr, ft = np.stack(r2), np.stack(nx2), np.stack(sr2), np.stack(ft2); acc = acc + np.stack(took)
    return {"yr": r.reshape(N, 128, V).astype(np.float32), "yf": ft.astype(np.float32), "yn": nx.astype(np.float32)}

@@ -1,0 +1,546 @@
+from concourse.mybir import AluOpType, ActivationFunctionType
+A = AluOpType
+F = ActivationFunctionType
+NK = 15
+BLOCKS = [("A", 0, 5), ("D", 5, 10), ("D", 10, 15)]
+RO = 3
+BIG = float(2 ** 21)
+NB = 3
+CY, GR, PC = 0.00083 * 1.2, 1.56, 0.00042 * 1.2
+ND = sum(b - a for p, a, b in BLOCKS if p == "D")
+
+SCRATCH = {}
+
+
+def _decl(names, shape, dtype, where="sbuf"):
+    for nm in names.split():
+        SCRATCH[nm] = (where, list(shape), dtype)
+
+
+_decl("pw", [128, 8192], "bfloat16")
+_decl("r32 mi", [128, 512], "int32")
+_decl("n32 s32 lbi opi opj ki bi cb wi wj", [128, 32], "int32")
+_decl("f32i", [8, 512], "int32")
+_decl("ff on8 of8", [8, 512], "float32")
+_decl("ob lg0 lg1 sg eh el obp dm", [128, 512], "bfloat16")
+_decl("en xx mq ms yrb k0 kd", [128, 512], "float32")
+_decl("pp", [128, 4, 128], "bfloat16")
+_decl("ora", [128, 4 * 1280], "bfloat16")
+_decl("lb opu um n1t", [128, 32], "uint16")
+_decl("zm uim", [128, 8, 4], "int32")
+_decl("tt kb m01 onf idf psf pqf", [128, 128], "float32")
+_decl("t8", [128, 64], "float32")
+_decl("t4 kk n1q n1s dn a1 nn wv e1 e2 g1 h1 l2 th hit nf", [128, 32], "float32")
+_decl("t2", [128, 16], "float32")
+_decl("ac", [128, 32], "bfloat16")
+_decl("oh", [128, 1024], "bfloat16")
+_decl("oha", [128, 2, 128], "bfloat16")
+_decl("dd", [128, 4, 4, 128], "bfloat16")
+_decl("x2", [128, 4, 8, 16], "bfloat16")
+_decl("an a8", [128, 8], "int32")
+_decl("qi", [128, 96], "float32")
+_decl("one", [128, 248], "bfloat16")
+_decl("g8f c8s", [128, 8], "float32")
+_decl("g8b g8h w0 w1 wsw", [128, 8], "bfloat16")
+_decl("bo nbo bo32 box idb nid wq psb pqb", [128, 128], "bfloat16")
+_decl("bw tga tha tgn thn tgm thm", [128, 8, 31], "bfloat16")
+_decl("wt", [128, 8, 15], "bfloat16")
+_decl("wgh wb", [128, 8, 15, 2], "bfloat16")
+_decl("wh wl", [128, 8, 16], "bfloat16")
+_decl("ci", [1, 256], "bfloat16")
+_decl("odd", [128, 4], "float32")
+_decl("sa me", [128, NB * 3840], "bfloat16")
+_decl("zi", [128, 4, 8, 2, 30], "int32")
+_decl("ui", [128, 4, 8, 60], "int32")
+_decl("uu", [128, 4 * 480], "uint16")
+_decl("qa", [128, 2, 2, 128], "bfloat16")
+_decl("pen", [128, 2, 4, 128], "bfloat16")
+_decl("rr lw sw so", [128, RO * 512], "bfloat16")
+_decl("tn", [128, RO * 32], "uint16")
+_decl("nx sr fx", [128, 4 * 32], "float32")
+_decl("kp0 kp1 kp2 ox0 ox1", [128, 512], "float32", "psum")
+_decl("px", [128, 2, 8, 32], "float32", "psum")
+_decl("ma mb", [128, 4, 128], "float32", "psum")
+
+PARTS = [(0, 256), (256, 384), (384, 512)]
+SEMAPHORES = ["qv", "qs", "qp", "qg", "ldr", "ldn", "ldo", "lds", "ldf", "ldp", "ldq", "ixm", "ls", "oy", "oz", "on", "of"]
+SEMAPHORES += ["ix%d" % i for i in range(4)] + ["al0"] + ["al%d%d" % (t, p) for t in (1, 2) for p in range(3)] + ["as%d" % t for t in range(3)]
+
+
+def build(g, T, core, topo):
+    ops = []
+    lastw, readers, bank = {}, {}, {}
+
+    def op(q, dur, fns, r=(), w=(), banks=(), sem=None, inc=0, lat=0.0, deps=()):
+        i = len(ops)
+        dp, soft = set(deps), set()
+        for k in r:
+            if k not in lastw:
+                raise ValueError("read before write " + k)
+            dp.add(lastw[k])
+        for k in w:
+            if k in lastw:
+                dp.add(lastw[k])
+            dp.update(readers.get(k, ()))
+        for k in r:
+            readers.setdefault(k, set()).add(i)
+        for k in w:
+            lastw[k] = i
+            readers[k] = set()
+        for b in banks:
+            st = bank.setdefault(b, {"e": None, "cur": [], "prev": []})
+            if st["e"] != q:
+                st["prev"], st["cur"], st["e"] = st["cur"], [], q
+            elif q == "p" and st["cur"]:
+                soft.add(st["cur"][-1])
+            dp.update(st["prev"])
+            st["cur"].append(i)
+        dp.discard(i)
+        ops.append({"q": q, "dur": dur, "fns": fns, "deps": dp, "soft": soft - dp, "sem": sem, "inc": inc, "lat": lat, "remote": False})
+        return i
+
+    def v(n, fn, r=(), w=(), banks=(), half=False):
+        fns = fn if isinstance(fn, list) else [fn]
+        return op("v", len(fns) * max(64, n * (0.5 if half else 1)) * CY, fns, r, w, banks)
+
+    def vg(n, fn, r=(), w=()):
+        return op("v", 0.05 + n * GR * CY, [fn], r, w)
+
+    def s(n, fn, r=(), w=(), banks=()):
+        fns = fn if isinstance(fn, list) else [fn]
+        return op("s", len(fns) * (0.03 + n * CY), fns, r, w, banks)
+
+    def sgt(n, fn, r=(), w=()):
+        return op("s", 0.065 + n * GR * CY, [fn], r, w)
+
+    def mm(out, lhsT, rhs, st, sp):
+        return lambda: g.tensor.matmul(out, lhsT, rhs, st, sp)
+
+    def pe(cyc, fns, r=(), w=(), banks=()):
+        return op("p", cyc * PC, fns, r, w, banks)
+
+    def gc(n, fn, r=(), w=()):
+        return op("g", 0.17 + 2 * n * CY, [fn], r, w)
+
+    tt, ts, tc, fill = g.vector.tensor_tensor, g.vector.tensor_scalar, g.vector.tensor_copy, g.vector.memset
+    act, sel = g.scalar.activation, g.affine_select
+    rank = T.rank_of(core)
+
+    def send(t, dst_t, src, sem_name, r, name):
+        p = T.cores[(rank - 1 - t % 7) % 8]
+        rid, pid, _ = topo.addr(p)
+        mask = 0
+        for e in topo.engines(core, p)[:8]:
+            mask |= 1 << e
+        i = op("g", 1.0, [lambda: g.remote_dma(dst_t, src, T.sem[sem_name], T.sem.ls, pid, rid, mask)], r, (), sem="ls", inc=8, lat=2.0)
+        ops[i]["remote"] = True
+        return op(None, 0.0, [], (), [name], deps=(i,), sem=sem_name, inc=8, lat=0.3)
+
+    def load(q, out, in_, sem, key, lat):
+        eng = g.sync if q == "y" else g.scalar
+        return op(q, 0.1, [lambda: eng.dma_start(out, in_)], (), [key], sem=sem, inc=16, lat=lat)
+    load("y", T.r32[:], T.resid[:], "ldr", "r32", 3.0)
+    load("s", T.n32[:], T.nx0[:], "ldn", "n32", 2.5)
+    load("s", T.s32[:], T.src0[:], "lds", "s32", 2.5)
+    load("s", T.ob[:], T.obs[:], "ldo", "ob", 3.0)
+    load("s", T.f32i[:], T.fit0[:], "ldf", "f32i", 3.0)
+    load("y", T.pw[:, 0:4096], T.prof[:, 0:4096], "ldp", "pw0", 8.0)
+    load("y", T.pw[:, 4096:8192], T.prof[:, 4096:8192], "ldq", "pw1", 11.0)
+    PW = ["pw0", "pw1"]
+    v(248, lambda: fill(T.one[:], 1.0), (), ["one"])
+    v(128, lambda: fill(T.onf[:], 1.0), (), ["onf"])
+    gc(120, lambda: sel(T.wt[:], T.one[:, 0:120], [[-16, 8], [0, 15]], A.is_ge, 0.0, 0, 1), ["one"], ["wtA"])
+    gc(120, lambda: sel(T.wt[:], T.wt[:], [[16, 8], [0, 15]], A.is_ge, 0.0, 15, -1), ["wtA"], ["wtB"])
+    v(120, lambda: tc(T.wb[:, :, :, 1], T.wt[:]), ["wtB"], ["wb1"])
+    v(120, lambda: fill(T.wb[:, :, :, 0], 0.0), (), ["wb0"])
+    gc(120, lambda: sel(T.wt[:], T.wt[:], [[16, 8], [1, 15]], A.is_ge, 0.0, 0, -1), ["wtB"], ["wtB", "wt"])
+    v(120, lambda: tc(T.wgh[:, :, :, 0], T.wt[:]), ["wt"], ["wgh0"])
+    v(240, lambda: tt(T.wgh[:, :, :, 1], T.wt[:], T.wb[:, :, :, 1], A.subtract), ["wt", "wb1"], ["wgh1"])
+    WGH, WB = ["wgh0", "wgh1"], ["wb0", "wb1"]
+    gc(4, lambda: g.iota(T.odd[:], [[256, 4]], 1, 2, allow_small_or_imprecise_dtypes=True), (), ["odd"])
+    gc(32, lambda: g.iota(T.lbi[:], [[1, 32]], 0, 0), (), ["lbi"])
+    v(32, lambda: tc(T.lb[:], T.lbi[:]), ["lbi"], ["lb"])
+    gc(512, lambda: g.iota(T.mi[:], [[0, 32], [-1, 16]], 0, 1), (), ["mi"])
+    v(512, lambda: ts(T.mi[:], T.mi[:], 15, None, A.bitwise_and), ["mi"], ["mi"])
+    v(512, lambda: ts(T.mq[:], T.mi[:], 0.0, None, A.is_equal), ["mi"], ["mq"])
+    gc(32, lambda: g.iota(T.opi[:], [[0, 4], [1, 8]], 0, 8), (), ["opi"])
+    gc(32, lambda: g.iota(T.opj[:], [[128, 4], [0, 8]], 0, 0), (), ["opj"])
+    v(32, lambda: ts(T.opi[:], T.opi[:], 127, None, A.bitwise_and), ["opi"], ["opi"])
+    v(64, lambda: tt(T.opj[:], T.opi[:], T.opj[:], A.add), ["opi", "opj"], ["opj"])
+    v(32, lambda: tc(T.opu[:], T.opj[:]), ["opj"], ["opu"])
+    gc(128, lambda: sel(T.bo[:], T.one[:, 0:128], [[-16, 8], [0, 16]], A.is_ge, 0.0, 0, 1), ["one"], ["bo_"])
+    gc(128, lambda: sel(T.bo[:], T.bo[:], [[16, 8], [0, 16]], A.is_ge, 0.0, 15, -1), ["bo_"], ["bo_", "bo"])
+    gc(8, lambda: sel(T.g8f[:], T.onf[:, 0:8], [[-16, 8]], A.is_ge, 0.0, 0, 1), ["onf"], ["g8_"])
+    gc(8, lambda: sel(T.g8f[:], T.g8f[:], [[16, 8]], A.is_ge, 0.0, 15, -1), ["g8_"], ["g8_", "g8f"])
+    v(8, lambda: tc(T.g8b[:], T.g8f[:]), ["g8f"], ["g8b"])
+    v(8, lambda: ts(T.g8h[:], T.g8f[:], 256.0, None, A.mult), ["g8f"], ["g8h"])
+    gc(128, lambda: sel(T.idf[:], T.onf[:], [[-1, 128]], A.is_equal, 0.0, 0, 1), ["onf"], ["idf"])
+    v(128, lambda: tc(T.idb[:], T.idf[:]), ["idf"], ["idb"])
+    v(128, lambda: ts(T.nid[:], T.idf[:], -1.0, None, A.mult), ["idf"], ["nid"])
+    v(256, lambda: tt(T.wq[:], T.idb[:], T.bo[:], A.subtract), ["idb", "bo"], ["wq"])
+    for nm, f in (("nbo", -1.0), ("bo32", 32.0), ("box", -32.0 * ND)):
+        v(128, (lambda nm=nm, f=f: ts(T[nm][:], T.bo[:], f, None, A.mult)), ["bo"], [nm], half=True)
+    gc(128, lambda: sel(T.psf[:], T.onf[:], [[-1, 16], [-16, 8]], A.is_equal, 0.0, 0, 1), ["onf"], ["psf"])
+    gc(128, lambda: sel(T.pqf[:], T.onf[:], [[-1, 8], [-8, 16]], A.is_equal, 0.0, 0, 1), ["onf"], ["pqf"])
+    v(128, lambda: tc(T.psb[:], T.psf[:]), ["psf"], ["psb"])
+    v(128, lambda: tc(T.pqb[:], T.pqf[:]), ["pqf"], ["pqb"])
+    gc(8, lambda: sel(T.w0[:], T.one[:, 0:8], [[-16, 8]], A.is_equal, 0.0, 0, 1), ["one"], ["w0"])
+    gc(8, lambda: sel(T.w1[:], T.one[:, 0:8], [[-16, 8]], A.is_equal, 0.0, -1, 1), ["one"], ["w1"])
+    v(8, lambda: ts(T.w0[:], T.w0[:], 256.0, None, A.mult), ["w0"], ["w0"])
+    v(16, lambda: tt(T.wsw[:], T.w0[:], T.w1[:], A.add), ["w0", "w1"], ["wsw"])
+    for x, nm in enumerate(("wh", "wl")):
+        v(128, (lambda nm=nm: fill(T[nm][:], 0.0)), (), [nm])
+        v(8, (lambda nm=nm, x=x: tc(T[nm][:, :, x], T.g8f[:])), ["g8f"], [nm])
+    gc(256, lambda: g.iota(T.ci[:], [[16, 2], [0, 8], [1, 16]], 32, 0, allow_small_or_imprecise_dtypes=True), (), ["ci"])
+    gc(248, lambda: sel(T.bw[:], T.one[:], [[-16, 8], [0, 31]], A.is_ge, 0.0, 0, 1), ["one"], ["bw_"])
+    gc(248, lambda: sel(T.bw[:], T.bw[:], [[16, 8], [0, 31]], A.is_ge, 0.0, 15, -1), ["bw_"], ["bw_", "bw"])
+    TK = {}
+    for nm, f in (("a", 32.0), ("n", -32.0), ("m", 64.0)):
+        TK[nm] = []
+        for tx, lo, hi in (("tg", 0.0, f), ("th", f, 0.0)):
+            for a, b, c in ((0, 15, lo), (15, 31, hi)):
+                v(8 * (b - a), (lambda tx=tx, nm=nm, a=a, b=b, c=c: ts(T[tx + nm][:, :, a:b], T.bw[:, :, a:b], c, None, A.mult)), ["bw"], [tx + nm + str(a)], half=True)
+                TK[nm].append(tx + nm + str(a))
+    v(128, lambda: fill(T.m01[:], 1.0), (), ["m01"])
+    v(8, lambda: fill(T.m01[:, 0:128:16], 0.0), (), ["m01"])
+    v(512, lambda: fill(T.kd[:], 0.0), (), ["kd%d" % c for c in range(4)])
+    v(512, lambda: fill(T.x2[:], 0.0), (), ["x2h", "x2l"])
+    v(8, lambda: fill(T.an[:], 0), (), ["an"])
+
+    v(512, lambda: tc(T.rr[:, 0:512], T.r32[:]), ["r32"], ["rr0_%d" % c for c in range(4)])
+    R0 = ["rr0_%d" % c for c in range(4)]
+    v(32, lambda: tc(T.tn[:, 0:32], T.n32[:]), ["n32"], ["tn0"])
+    send(0, T.lw[:, 0:512], T.rr[:, 0:512], "al0", R0, "lw0_0")
+    v(32, lambda: ts(T.hit[:], T.s32[:], 256.0, None, A.is_ge), ["s32"], ["hit"])
+    v(32, lambda: ts(T.l2[:], T.hit[:], -256.0, None, A.mult), ["hit"], ["l2"])
+    v(64, lambda: tt(T.l2[:], T.l2[:], T.s32[:], A.add), ["l2", "s32"], ["l2"])
+    LB = T.lb[:, 0:32]
+    vg(512, lambda: tt(T.eh[:], T.hit[:, 0:32].indirect(LB), T.mq[:], A.mult), ["hit", "lb", "mq"], ["eh"])
+    vg(512, lambda: tt(T.el[:], T.l2[:, 0:32].indirect(LB), T.mq[:], A.mult), ["l2", "lb", "mq"], ["el"])
+    pe(1024, [f for c in range(4) for f in (mm(T.mb[:, c, :], T.wh[:], T.eh[:, 128 * c:128 * c + 128], True, False),
+                                            mm(T.mb[:, c, :], T.wl[:], T.el[:, 128 * c:128 * c + 128], False, True))], ["wh", "wl", "eh", "el"], (), ["mb"])
+
+    def copy4(dst, o, key, bk="mb", rows=128):
+        s(128, [(lambda c=c: act(dst[0:rows, o + 128 * c:o + 128 * c + 128], T[bk][0:rows, c, :], F.Copy)) for c in range(4)], (), [key], [bk])
+    copy4(T.so, 0, "so0")
+    send(0, T.sw[:, 0:512], T.so[:, 0:512], "as0", ["so0"], "sw0")
+
+    vg(512, lambda: tc(T.obp[:], T.ob[:, 0:512].indirect(T.opu[:, 0:32])), ["ob", "opu"], ["obp"])
+    for c in range(4):
+        for lo, hi in ((0, 128), (128, 256), (256, 512), (512, 1024), (1024, 1280)):
+            src = (T.obp, 128 * c, "obp") if hi <= 256 else (T.ora, 1280 * c, "ora%d" % c)
+            v(hi - lo, (lambda c=c, lo=lo, hi=hi, src=src: tc(T.ora[:, 1280 * c + lo:1280 * c + hi], src[0][:, src[1]:src[1] + hi - lo])),
+              ["obp"] + ([src[2]] if hi > 256 else []), ["ora%d" % c], half=True)
+        for r in range(2):
+            o = 256 * (c % 2) + 128 * r
+            v(128, (lambda c=c, o=o: tc(T["ox%d" % (c // 2)][:, o:o + 128], T.obp[:, 128 * c:128 * c + 128])), ["obp"], ["ox%d%d" % (c, r)])
+
+    def rrs(t, ch):
+        return T.rr[:, t * 512 + ch * 128:t * 512 + ch * 128 + 128]
+
+    def own_mass():
+        pe(256, [mm(T.ma[:, 0, 8 * c:8 * c + 8], rrs(0, c), T.g8b[:], True, True) for c in range(4)], R0 + ["g8b"], (), ["ma"])
+        v(8, [(lambda c=c: ts(T.zm[:, :, c], T.ma[:, 0, 8 * c:8 * c + 8], 4096.0, T.odd[:, c:c + 1], A.add, A.mult)) for c in range(4)], ["odd"], ["zm"], ["ma"])
+        v(32, lambda: ts(T.zm[:], T.zm[:], 1, 8191, A.arith_shift_right, A.bitwise_and), ["zm"], ["zm"])
+        op("y", 0.6, [(lambda k=k: g.sync.dma_start(T.uim[16 * k:16 * k + 16, :, :], T.zm[:, k, :])) for k in range(8)], ["zm"], ["uim"], sem="ixm", inc=128, lat=2.5)
+        v(4, [(lambda b=b: tc(T.um[:, b:32:8], T.uim[:, b, :])) for b in range(8)], ["uim"], ["um"])
+        vg(512, lambda: tt(T.dm[:], T.pw[:, 0:8192].indirect(T.um[:, 0:32]), T.obp[:], A.subtract), PW + ["um", "obp"], ["dm"])
+        s(512, lambda: act(T.dm[:], T.dm[:], F.Abs), ["dm"], ["dm"])
+
+    def init_scalars():
+        v(32, lambda: tc(T.nf[:], T.n32[:]), ["n32"], ["nf"])
+        vg(512, lambda: tt(T.en[:], T.nf[:, 0:32].indirect(LB), T.mq[:], A.mult), ["nf", "lb", "mq"], ["en"])
+        op("v", 512 * CY, [lambda: tc(T.ff[:], T.f32i[:])], ["f32i"], ["ff"])
+        fns = []
+        for c in range(4):
+            sl = slice(c * 128, c * 128 + 128)
+            fns += [mm(T.mb[:, 0, 8 * c:8 * c + 8], T.en[:, sl], T.g8f[:], True, True),
+                    mm(T.mb[:, 0, 32 + 8 * c:40 + 8 * c], T.eh[:, sl], T.g8h[:], True, False),
+                    mm(T.mb[:, 0, 32 + 8 * c:40 + 8 * c], T.el[:, sl], T.g8b[:], False, True),
+                    mm(T.mb[:, 0, 64 + 8 * c:72 + 8 * c], T.ff[0:8, sl], T.idf[0:8, 0:8], True, True)]
+        pe(40 * 64, fns, ["en", "eh", "el", "ff", "g8f", "g8b", "g8h", "idf"], (), ["mb"])
+        v(96, lambda: tc(T.qi[:], T.mb[:, 0, 0:96]), (), ["qi"], ["mb"])
+        pe(512, [mm(T.mb[:, 1, 0:96], T.pqf[:], T.qi[:], True, True)], ["pqf", "qi"], (), ["mb"])
+        v(32, lambda: tc(T.nx[:, 0:32], T.mb[:, 1, 0:32]), (), ["nx0"], ["mb"])
+        v(32, lambda: tc(T.sr[:, 0:32], T.mb[:, 1, 32:64]), (), ["sr0"], ["mb"])
+        v(32, lambda: ts(T.fx[:, 0:32], T.mb[:, 1, 64:96], 1.0, None, A.add), (), ["fx0"], ["mb"])
+        v(32, lambda: ts(T.th[:], T.fx[:, 0:32], 32.0, None, A.mult), ["fx0"], ["th"])
+        pe(2048 + 256, [mm(T.mb[:, c, :], T.pqf[:], T.mq[:, 128 * c:128 * c + 128], True, True) for c in range(4)], ["pqf", "mq"], (), ["mb"])
+        copy4(T.ms, 0, "ms")
+        pe(256, [mm(T.mb[:, 0, 0:8], T.pqf[:], T.g8f[:], True, True)], ["pqf", "g8f"], (), ["mb"])
+        v(8, lambda: tc(T.c8s[:], T.mb[:, 0, 0:8]), (), ["c8s"], ["mb"])
+
+    LG = [T.lg0, T.lg1]
+    nscore = [0]
+
+    def gather_lists(t, c):
+        tk = "tn%d" % t if c == 0 else "n1t"
+        win = T.lw[:, 512 * t:512 * t + 512]
+        lws = ["lw%d_%d" % (t, p) for p in range(1 if t == 0 else 3)]
+        for h in range(2):
+            idx = T.tn[:, 32 * t + 16 * h:32 * t + 16 * h + 16] if c == 0 else T.n1t[:, 16 * h:16 * h + 16]
+            o = LG[c][:, 256 * h:256 * h + 256]
+            if h == 0 and c == 0:
+                vg(256, (lambda o=o, idx=idx: tc(o, win.indirect(idx))), lws + [tk], ["lg%d%d" % (c, h)])
+            else:
+                sgt(256, (lambda o=o, idx=idx: act(o, win.indirect(idx), F.Copy)), lws + [tk], ["lg%d%d" % (c, h)])
+
+    def index(t, c, h):
+        lk, i = "lg%d%d" % (c, h), 2 * c + h
+        zk = "zi%d" % i
+        fns = []
+        for e in range(2):
+            ch = 2 * h + e
+            fns += [mm(T.px[:, e, :, 0:30], LG[c][:, ch * 128:ch * 128 + 128], T.wgh[:], True, False),
+                    mm(T.px[:, e, :, 0:30], rrs(0, ch), T.wb[:], False, True)]
+        pe(960, fns, [lk] + WGH + WB + R0, (), ["px"])
+        v(240, [(lambda e=e: ts(T.zi[:, i, :, e, :], T.px[:, e, :, 0:30], 4096.0, T.odd[:, 2 * h + e:2 * h + e + 1], A.add, A.mult)) for e in range(2)], ["odd"], [zk], ["px"])
+        v(480, lambda: ts(T.zi[:, i], T.zi[:, i], 1, 8191, A.arith_shift_right, A.bitwise_and), [zk], [zk])
+        op("y", 0.6, [(lambda k=k: g.sync.dma_start(T.ui[16 * k:16 * k + 16, i, :, :], T.zi[:, i, k, :, :])) for k in range(8)], [zk], ["ui%d" % i], sem="ix%d" % i, inc=128, lat=3.0)
+        v(60, [(lambda b=b: tc(T.uu[:, 480 * i + b:480 * i + 480:8], T.ui[:, i, b, :])) for b in range(8)], ["ui%d" % i], ["uu%d" % i])
+
+    def pen(t, c, h):
+        fns = []
+        for e in range(2):
+            ch = 2 * h + e
+            fns += [mm(T.ma[:, e, :], LG[c][:, ch * 128:ch * 128 + 128], T.wq[:], True, False), mm(T.ma[:, e, :], rrs(0, ch), T.bo[:], False, True)]
+        pe(512, fns, ["lg%d%d" % (c, h), "wq", "bo"] + R0, (), ["ma"])
+        s(256, lambda: act(T.qa[:, c], T.ma[:, 0:2, :], F.Abs, bias=-127.5), (), ["qa%d" % c], ["ma"])
+        v(256, lambda: ts(T.pen[:, c, 2 * h:2 * h + 2, :], T.qa[:, c], 127.5, BIG, A.is_gt, A.mult), ["qa%d" % c], ["pen%d%d" % (c, h)], half=True)
+
+    def dld(t, c, h):
+        hs = slice(256 * h, 256 * h + 256)
+        rk = ["rr%d_%d" % (t, 2 * h), "rr%d_%d" % (t, 2 * h + 1)]
+        rt = T.rr[:, t * 512 + 256 * h:t * 512 + 256 * h + 256]
+        pe(1024, [mm(T.ma[:, 0:2, :], T.idb[:], LG[c][:, hs], True, False), mm(T.ma[:, 0:2, :], T.nid[:], rt, False, True),
+                  mm(T.ma[:, 2:4, :], T.nbo[:], LG[c][:, hs], True, False), mm(T.ma[:, 2:4, :], T.bo[:], T.rr[:, hs], False, True)],
+           ["lg%d%d" % (c, h), "idb", "nid", "nbo", "bo"] + rk + R0, (), ["ma"])
+        for x in range(2):
+            s(256, (lambda x=x: act(T.dd[:, 2 * h:2 * h + 2, 2 * x + c, :], T.ma[:, 2 * x:2 * x + 2, :], F.Copy)), (), ["dd%d%d%d" % (c, h, x)], ["ma"])
+
+    def n1_chain(t):
+        sgt(512, lambda: act(T.sg[:], T.sw[:, 512 * t:512 * t + 512].indirect(T.tn[:, 32 * t:32 * t + 32]), F.Copy), ["sw%d" % t, "tn%d" % t], ["sg"])
+        pe(256, [mm(T.ma[:, 0, 8 * c:8 * c + 8], T.sg[:, 128 * c:128 * c + 128], T.wsw[:], True, True) for c in range(4)], ["sg", "wsw"], (), ["ma"])
+        v(32, lambda: tc(T.n1q[:], T.ma[:, 0, 0:32]), (), ["n1q"], ["ma"])
+        vg(512, lambda: tt(T.xx[:], T.n1q[:, 0:32].indirect(LB), T.mq[:], A.mult), ["n1q", "lb", "mq"], ["xx"])
+        pe(1280, [mm(T.ma[:, 1, 8 * c:8 * c + 8], T.xx[:, 128 * c:128 * c + 128], T.g8f[:], True, True) for c in range(4)] +
+           [mm(T.ma[:, 1, 32:64], T.pqf[:], T.n1q[:], True, True)], ["xx", "g8f", "pqf", "n1q"], (), ["ma"])
+        v(32, lambda: tc(T.n1t[:], T.ma[:, 1, 0:32]), (), ["n1t"], ["ma"])
+        v(32, lambda: tc(T.n1s[:], T.ma[:, 1, 32:64]), (), ["n1s"], ["ma"])
+        v(64, lambda: tt(T.dn[:], T.n1s[:], T.nx[:, 32 * t:32 * t + 32], A.subtract), ["n1s", "nx%d" % t], ["dn"])
+
+    def wsl(nm, kd, k):
+        return T[("th" if kd else "tg") + nm][:, :, 14 - k:30 - k]
+
+    def score(t, c, ch):
+        h, e = ch // 2, ch % 2
+        i = 2 * c + h
+        b, kn = 3840 * (nscore[0] % NB), "kp%d" % (nscore[0] % 3)
+        nscore[0] += 1
+        key, c0, WIN = T[kn][:, 0:128], 480 * i + 240 * e, T.pw[:, 0:8192]
+        for p, ka, kb in BLOCKS:
+            n = 256 * (kb - ka)
+            off = T.uu[:, c0 + 16 * ka:c0 + 16 * kb]
+            o, sk, mk = T.sa[:, b + 256 * ka:b + 256 * kb], "sa%d_%d" % (b, ka), "me%d_%d" % (b, ka)
+            if p == "A":
+                vg(n, (lambda o=o, off=off, n=n: tt(o, WIN.indirect(off), T.ora[:, 1280 * ch:1280 * ch + n], A.subtract)), PW + ["uu%d" % i, "ora%d" % ch], [sk])
+                s(n, (lambda o=o: act(o, o, F.Abs)), [sk], [sk])
+            else:
+                sgt(n, (lambda o=o, off=off: act(o, WIN.indirect(off), F.Copy)), PW + ["uu%d" % i], [sk])
+                v(256, [(lambda x=b + 256 * x: tt(T.me[:, x:x + 256], T.sa[:, x:x + 256], T["ox%d" % h][:, 256 * e:256 * e + 256], A.max)) for x in range(ka, kb)],
+                  [sk, "ox%d0" % ch, "ox%d1" % ch], [mk])
+        pe(512, [mm(key, T.pqb[:], T.pen[:, c, ch, :], True, False), mm(key, T.one[0:1, 0:128], T.ci[0:1, 128 * c:128 * c + 128], False, False),
+                 mm(key, T.obp[:, 128 * ch:128 * ch + 128], T.box[:], False, False), mm(key, T.dm[:, 128 * ch:128 * ch + 128], T.bo32[:], False, False)],
+           ["pqb", "pen%d%d" % (c, h), "one", "ci", "obp", "box", "dm", "bo32"], (), [kn])
+        jobs = [(p, ka, kb, "a" if p == "A" else "n") for p, ka, kb in BLOCKS] + [(p, ka, kb, "m") for p, ka, kb in BLOCKS if p == "D"]
+        for z, (p, ka, kb, nm) in enumerate(jobs):
+            buf, bk = (T.me, "me") if nm == "m" else (T.sa, "sa")
+            ks = [(k, kd) for k in range(ka, kb) for kd in range(2)]
+            pe(128 * len(ks), [mm(key, buf[:, b + 256 * k + 128 * kd:b + 256 * k + 128 * kd + 128], wsl(nm, kd, k), False, z == len(jobs) - 1 and (k, kd) == ks[-1]) for k, kd in ks],
+               ["%s%d_%d" % (bk, b, ka)] + TK[nm], (), [kn])
+        return kn
+
+    def tail(t, ch, kn):
+        h, key, c128, k8 = ch // 2, T[kn][:, 0:128], slice(128 * ch, 128 * ch + 128), slice(8 * ch, 8 * ch + 8)
+        k0, oh = T.k0[:, c128], [T.oh[:, 256 * ch + 128 * c:256 * ch + 128 * c + 128] for c in range(2)]
+        v(128, lambda: tt(T.tt[:], key, k0, A.min), ["k0%d" % ch], ["tt"], [kn])
+        v(128, lambda: tt(T.t8[:], T.tt[:, 0:128:2], T.tt[:, 1:128:2], A.min), ["tt"], ["t8"])
+        v(64, lambda: tt(T.t4[:], T.t8[:, 0:64:2], T.t8[:, 1:64:2], A.min), ["t8"], ["t4"])
+        v(32, lambda: tt(T.t2[:], T.t4[:, 0:32:2], T.t4[:, 1:32:2], A.min), ["t4"], ["t2"])
+        v(16, lambda: tt(T.kk[:, k8], T.t2[:, 0:16:2], T.t2[:, 1:16:2], A.min), ["t2"], ["kk%d" % ch])
+        v(16, lambda: tt(T.ac[:, k8], T.kk[:, k8], T.th[:, k8], A.is_lt), ["kk%d" % ch, "th"], ["ac%d" % ch])
+        v(16, lambda: tt(T.kd[:, 128 * ch:128 * ch + 128:16], T.kk[:, k8], T.ac[:, k8], A.mult), ["kk%d" % ch, "ac%d" % ch], ["kd%d" % ch])
+        v(128, lambda: g.vector.tensor_tensor_scan(T.kb[:], T.m01[:], T.kd[:, c128], 0.0, A.mult, A.add), ["m01", "kd%d" % ch], ["kb"])
+        v(128, lambda: tt(oh[1], key, T.kb[:], A.is_equal), ["kb"], ["oh1%d" % ch], [kn])
+        v(256, lambda: tt(oh[0], k0, T.kb[:], A.is_equal), ["kb", "k0%d" % ch], ["oh0%d" % ch])
+        pe(256, [mm(T.mb[:, c, :], oh[c], T.psb[:], True, True) for c in range(2)], ["oh0%d" % ch, "oh1%d" % ch, "psb"], (), ["mb"])
+        s(256, lambda: act(T.oha[:], T.mb[:, 0:2, :], F.Copy), (), ["oha"], ["mb"])
+        pe(512, [mm(T.mb[:, 0:2, :], T.bo[:], T.oha[:], True, True), mm(T.mb[:, 2:4, :], T.idb[:], T.oha[:], True, True)], ["bo", "idb", "oha"], (), ["mb"])
+        v(512, lambda: tt(T.pp[:], T.mb[:], T.dd[:, ch], A.mult), ["dd%d%d%d" % (c, h, x) for c in range(2) for x in range(2)], ["pp"], ["mb"])
+        pe(640, [mm(T.mb[:, 0, :], T.idb[:], rrs(t, ch), True, False)] + [mm(T.mb[:, 0, :], T.idb[:], T.pp[:, x, :], False, x == 3) for x in range(4)],
+           ["idb", "rr%d_%d" % (t, ch), "pp"], (), ["mb"])
+        if t < RO - 1:
+            s(128, lambda: act(rrs(t + 1, ch), T.mb[:, 0, :], F.Copy), (), ["rr%d_%d" % (t + 1, ch)], ["mb"])
+        else:
+            s(128, lambda: act(T.yrb[:, c128], T.mb[:, 0, :], F.Copy), (), ["yrb%d" % ch], ["mb"])
+
+    def scalars(t):
+        o, n = slice(32 * t, 32 * t + 32), slice(32 * t + 32, 32 * t + 64)
+        kks, acs = ["kk%d" % c for c in range(4)], ["ac%d" % c for c in range(4)]
+        v(32, lambda: tc(T.ki[:], T.kk[:]), kks, ["ki"])
+        v(32, lambda: ts(T.cb[:], T.ki[:], 4, 1, A.arith_shift_right, A.bitwise_and), ["ki"], ["cb"])
+        v(32, lambda: ts(T.bi[:], T.ki[:], 5, None, A.arith_shift_right), ["ki"], ["bi"])
+        v(64, lambda: tt(T.a1[:], T.cb[:], T.dn[:], A.mult), ["cb", "dn"], ["a1"])
+        v(64, lambda: tt(T.nn[:], T.a1[:], T.nx[:, o], A.add), ["a1", "nx%d" % t], ["nn"])
+        v(32, lambda: ts(T.wv[:], T.nn[:], 13.0, -1.0, A.mult, A.add), ["nn"], ["wv"])
+        v(64, lambda: tt(T.wi[:], T.wv[:], T.bi[:], A.add), ["wv", "bi"], ["wi"])
+        v(32, lambda: ts(T.wj[:], T.wi[:], 511, None, A.bitwise_and), ["wi"], ["wj"])
+        v(64, lambda: tt(T.e1[:], T.wj[:], T.n1s[:], A.subtract), ["wj", "n1s"], ["e1"])
+        v(64, lambda: tt(T.e2[:], T.e1[:], T.ac[:], A.mult), ["e1"] + acs, ["e2"])
+        v(64, lambda: tt(T.nx[:, n], T.e2[:], T.n1s[:], A.add), ["e2", "n1s"], ["nx%d" % (t + 1)])
+        if t < RO - 1:
+            vg(512, lambda: tt(T.xx[:], T.nx[:, n].indirect(LB), T.ms[:], A.mult), ["nx%d" % (t + 1), "lb", "ms"], ["xx"])
+            pe(1024, [mm(T.mb[:, 1, 8 * c:8 * c + 8], T.xx[:, 128 * c:128 * c + 128], T.c8s[:], True, True) for c in range(4)], ["xx", "c8s"], (), ["mb"])
+            v(32, lambda: tc(T.tn[:, 32 * t + 32:32 * t + 64], T.mb[:, 1, 0:32]), (), ["tn%d" % (t + 1)], ["mb"])
+            v(64, lambda: tt(T.h1[:], T.nn[:], T.sr[:, o], A.subtract), ["nn", "sr%d" % t], ["h1"])
+            v(64, lambda: tt(T.h1[:], T.h1[:], T.ac[:], A.mult), ["h1"] + acs, ["h1"])
+            v(64, lambda: tt(T.sr[:, n], T.h1[:], T.sr[:, o], A.add), ["h1", "sr%d" % t], ["sr%d" % (t + 1)])
+            v(32, lambda: ts(T.l2[:], T.sr[:, n], 256.0, -256.0, A.is_ge, A.mult), ["sr%d" % (t + 1)], ["l2"])
+            XK = []
+            for ch in range(4):
+                k8, n8 = slice(8 * ch, 8 * ch + 8), slice(32 * t + 32 + 8 * ch, 32 * t + 40 + 8 * ch)
+                v(8, (lambda ch=ch, n8=n8: ts(T.x2[:, ch, :, 0], T.sr[:, n8], 256.0, None, A.is_ge)), ["sr%d" % (t + 1), "x2h"], ["x2h%d" % ch])
+                v(16, (lambda ch=ch, n8=n8, k8=k8: tt(T.x2[:, ch, :, 1], T.l2[:, k8], T.sr[:, n8], A.add)), ["sr%d" % (t + 1), "l2", "x2l"], ["x2l%d" % ch])
+                XK += ["x2h%d" % ch, "x2l%d" % ch]
+            pe(512, [mm(T.mb[:, c, :], T.x2[:, c], T.psb[:], True, True) for c in range(4)], XK + ["psb"], (), ["mb"])
+            copy4(T.so, 512 * t + 512, "so%d" % (t + 1))
+        v(64, lambda: tt(T.g1[:], T.bi[:], T.fx[:, o], A.subtract), ["bi", "fx%d" % t], ["g1"])
+        v(64, lambda: tt(T.g1[:], T.g1[:], T.ac[:], A.mult), ["g1"] + acs, ["g1"])
+        v(64, lambda: tt(T.fx[:, n], T.g1[:], T.fx[:, o], A.add), ["g1", "fx%d" % t], ["fx%d" % (t + 1)])
+
+    def thresholds(t):
+        n = 32 * t + 32
+        acs = ["ac%d" % c for c in range(4)]
+        pe(256, [mm(T.ma[:, 0, 0:8], T.one[:, 0:128], T.ac[:, 8 * c:8 * c + 8], c == 0, c == 3) for c in range(4)], ["one"] + acs, (), ["ma"])
+        v(16, lambda: tt(T.an[:], T.ma[:, 0, 0:8], T.an[:], A.add), ["an"], ["an"], ["ma"])
+        v(8, lambda: ts(T.a8[:], T.an[:], 7, None, A.bitwise_and), ["an"], ["a8"])
+        v(16, [(lambda c=c: tt(T.e1[:, 8 * c:8 * c + 8], T.fx[:, n + 8 * c:n + 8 * c + 8], T.a8[:], A.subtract)) for c in range(4)], ["fx%d" % (t + 1), "a8"], ["e1"])
+        v(32, lambda: ts(T.th[:], T.e1[:], 32.0, None, A.mult), ["e1"], ["th"])
+
+    for t in range(RO):
+        gather_lists(t, 0)
+        index(t, 0, 0)
+        pen(t, 0, 0)
+        if t == 0:
+            own_mass()
+            init_scalars()
+        n1_chain(t)
+        index(t, 0, 1)
+        pen(t, 0, 1)
+        if t > 0:
+            thresholds(t - 1)
+        gather_lists(t, 1)
+        for h in range(2):
+            index(t, 1, h)
+            pen(t, 1, h)
+        for h in range(2):
+            for c in range(2):
+                dld(t, c, h)
+        for c, ch in [(0, 0), (0, 1), (1, 0), (1, 1), (0, 2), (1, 2), (0, 3), (1, 3)]:
+            kn = score(t, c, ch)
+            if c == 0:
+                s(128, (lambda kn=kn, ch=ch: act(T.k0[:, 128 * ch:128 * ch + 128], T[kn][:, 0:128], F.Copy)), (), ["k0%d" % ch], [kn])
+                continue
+            tail(t, ch, kn)
+            if t < RO - 1 and ch > 0:
+                lo, hi = PARTS[ch - 1]
+                o = 512 * (t + 1)
+                send(t + 1, T.lw[:, o + lo:o + hi], T.rr[:, o + lo:o + hi], "al%d%d" % (t + 1, ch - 1),
+                     ["rr%d_%d" % (t + 1, x) for x in range(lo // 128, hi // 128)], "lw%d_%d" % (t + 1, ch - 1))
+        scalars(t)
+        if t < RO - 1:
+            o = 512 * (t + 1)
+            send(t + 1, T.sw[:, o:o + 512], T.so[:, o:o + 512], "as%d" % (t + 1), ["so%d" % (t + 1)], "sw%d" % (t + 1))
+    op("y", 0.1, [lambda: g.sync.dma_start(T.yr[:, 0:384], T.yrb[:, 0:384])], ["yrb0", "yrb1", "yrb2"], (), sem="oy", inc=16, lat=2.0)
+    op("y", 0.1, [lambda: g.sync.dma_start(T.yr[:, 384:512], T.yrb[:, 384:512])], ["yrb3"], (), sem="oz", inc=16, lat=2.0)
+    pe(4 * 512, [mm(T.ma[0:8, c, :], T.nx[:, 96 + 8 * c:104 + 8 * c], T.psf[:], True, True) for c in range(4)], ["nx3", "psf"], (), ["ma"])
+    copy4(T.on8, 0, "on8", "ma", 8)
+    op("y", 0.1, [lambda: g.sync.dma_start(T.yn[:], T.on8[:])], ["on8"], (), sem="on", inc=16, lat=2.0)
+    pe(4 * 512, [mm(T.mb[0:8, c, :], T.fx[:, 96 + 8 * c:104 + 8 * c], T.psf[:], True, True) for c in range(4)], ["fx3", "psf"], (), ["mb"])
+    v(128, [(lambda c=c: ts(T.of8[:, 128 * c:128 * c + 128], T.mb[0:8, c, :], -1.0, None, A.add)) for c in range(4)], (), ["of8"], ["mb"])
+    op("y", 0.1, [lambda: g.sync.dma_start(T.yf[:], T.of8[:])], ["of8"], (), sem="of", inc=16, lat=2.0)
+    return ops
+
+
+def schedule(ops):
+    n = len(ops)
+    succ = [[] for _ in range(n)]
+    for i, o in enumerate(ops):
+        for d in o["deps"] | o["soft"]:
+            succ[d].append(i)
+    prio = [0.0] * n
+    for i in range(n - 1, -1, -1):
+        prio[i] = ops[i]["dur"] + ops[i]["lat"] + max([prio[j] for j in succ[i]], default=0.0)
+    left = [len(o["deps"] | o["soft"]) for o in ops]
+    fin, ready, free, busy = [0.0] * n, [0.0] * n, {}, {}
+    avail = [i for i in range(n) if left[i] == 0]
+    order = []
+    while avail:
+        best = None
+        for i in avail:
+            q = ops[i]["q"]
+            st = max(ready[i], free.get(q, 0.0)) if q else ready[i]
+            k = (round(st, 3), -prio[i])
+            if best is None or k < best[0]:
+                best = (k, i, st)
+        _, i, st = best
+        avail.remove(i)
+        o = ops[i]
+        if o["q"]:
+            free[o["q"]] = st + o["dur"]
+            busy[o["q"]] = busy.get(o["q"], 0.0) + o["dur"]
+        fin[i] = st + o["dur"] + o["lat"]
+        order.append((st, i))
+        for j in succ[i]:
+            left[j] -= 1
+            rt = st + o["dur"] if i in ops[j]["soft"] else fin[i] + (0.05 if ops[j]["q"] == o["q"] else 0.1)
+            ready[j] = max(ready[j], rt)
+            if left[j] == 0:
+                avail.append(j)
+    return order, fin, busy
+
+
+def rank_program(g, core, T, topo):
+    if T.rank_of(core) is None:
+        return
+    ops = build(g, T, core, topo)
+    order = schedule(ops)[0]
+    queue = {"v": g.vector, "s": g.scalar, "p": g.tensor, "g": g, "y": g.sync}
+    own = {"v": "qv", "s": "qs", "p": "qp", "g": "qg"}
+    count, known, ev, clock = {}, {}, {}, {}
+    for st, i in order:
+        o = ops[i]
+        q = o["q"]
+        if q is None:
+            count[o["sem"]] = count.get(o["sem"], 0) + o["inc"]
+            ev[i], clock[i] = (o["sem"], count[o["sem"]]), {}
+            continue
+        kn = known.setdefault(q, {})
+        for d in sorted(o["deps"], reverse=True):
+            sm, val = ev[d]
+            if kn.get(sm, 0) < val:
+                queue[q].wait_ge(T.sem[sm], val)
+                kn[sm] = val
+                for a, b in clock[d].items():
+                    kn[a] = max(kn.get(a, 0), b)
+        sm = o["sem"] or own[q]
+        step = o["inc"] // len(o["fns"]) if o["sem"] else 1
+        for fn in o["fns"]:
+            ins = fn()
+            if not o["remote"]:
+                ins.then_inc(T.sem[sm], step)
+            count[sm] = count.get(sm, 0) + step
+        ev[i], clock[i] = (sm, count[sm]), dict(kn)
+    for sm in sorted(count):
+        if known.get("g", {}).get(sm, 0) < count[sm]:
+            g.wait_ge(T.sem[sm], count[sm])

@@ -2,12 +2,12 @@ from concourse.mybir import AluOpType, ActivationFunctionType
 A = AluOpType
 F = ActivationFunctionType
 NK = 15
-BLOCKS = [("A", 0, 5), ("D", 5, 10), ("D", 10, 15)]
+BLOCKS = [("E", 0, 4), ("E", 4, 8), ("A", 8, 12), ("B", 12, 15)]
 RO = 3
 BIG = float(2 ** 21)
-NB = 3
-CY, GR, PC = 0.00083 * 1.2, 1.56, 0.00042 * 1.2
-ND = sum(b - a for p, a, b in BLOCKS if p == "D")
+NB, NKP = 3, 4
+CY, GR, PC, EO, EL = 0.00083 * 1.15, 1.5, 0.00042 * 1.15, 1.0, 3.0
+ALPHA = 150.0
 
 SCRATCH = {}
 
@@ -25,7 +25,7 @@ _decl("ff on8 of8", [8, 512], "float32")
 _decl("ob lg0 lg1 sg eh el obp dm", [128, 512], "bfloat16")
 _decl("en xx mq ms yrb k0 kd", [128, 512], "float32")
 _decl("pp", [128, 4, 128], "bfloat16")
-_decl("ora", [128, 4 * 1280], "bfloat16")
+_decl("ora nra", [128, 4 * 1024], "bfloat16")
 _decl("lb opu um n1t", [128, 32], "uint16")
 _decl("zm uim", [128, 8, 4], "int32")
 _decl("tt kb m01 onf idf psf pqf", [128, 128], "float32")
@@ -42,7 +42,7 @@ _decl("qi", [128, 96], "float32")
 _decl("one", [128, 248], "bfloat16")
 _decl("g8f c8s", [128, 8], "float32")
 _decl("g8b g8h w0 w1 wsw", [128, 8], "bfloat16")
-_decl("bo nbo bo32 box idb nid wq psb pqb", [128, 128], "bfloat16")
+_decl("bo nbo bo32 idb nid wq psb pqb", [128, 128], "bfloat16")
 _decl("bw tga tha tgn thn tgm thm", [128, 8, 31], "bfloat16")
 _decl("wt", [128, 8, 15], "bfloat16")
 _decl("wgh wb", [128, 8, 15, 2], "bfloat16")
@@ -58,13 +58,14 @@ _decl("pen", [128, 2, 4, 128], "bfloat16")
 _decl("rr lw sw so", [128, RO * 512], "bfloat16")
 _decl("tn", [128, RO * 32], "uint16")
 _decl("nx sr fx", [128, 4 * 32], "float32")
-_decl("kp0 kp1 kp2 ox0 ox1", [128, 512], "float32", "psum")
+_decl("kp0 kp1 kp2 kp3", [128, 512], "float32", "psum")
 _decl("px", [128, 2, 8, 32], "float32", "psum")
-_decl("ma mb", [128, 4, 128], "float32", "psum")
+_decl("ma mb mc", [128, 4, 128], "float32", "psum")
 
 PARTS = [(0, 256), (256, 384), (384, 512)]
 SEMAPHORES = ["qv", "qs", "qp", "qg", "ldr", "ldn", "ldo", "lds", "ldf", "ldp", "ldq", "ixm", "ls", "oy", "oz", "on", "of"]
 SEMAPHORES += ["ix%d" % i for i in range(4)] + ["al0"] + ["al%d%d" % (t, p) for t in (1, 2) for p in range(3)] + ["as%d" % t for t in range(3)]
+SEMAPHORES += ["e%d_%d" % (b, ka) for b in range(NB) for p, ka, kb in BLOCKS if p == "E"]
 
 
 def build(g, T, core, topo):
@@ -178,7 +179,7 @@ def build(g, T, core, topo):
     v(128, lambda: tc(T.idb[:], T.idf[:]), ["idf"], ["idb"])
     v(128, lambda: ts(T.nid[:], T.idf[:], -1.0, None, A.mult), ["idf"], ["nid"])
     v(256, lambda: tt(T.wq[:], T.idb[:], T.bo[:], A.subtract), ["idb", "bo"], ["wq"])
-    for nm, f in (("nbo", -1.0), ("bo32", 32.0), ("box", -32.0 * ND)):
+    for nm, f in (("nbo", -1.0), ("bo32", 32.0)):
         v(128, (lambda nm=nm, f=f: ts(T[nm][:], T.bo[:], f, None, A.mult)), ["bo"], [nm], half=True)
     gc(128, lambda: sel(T.psf[:], T.onf[:], [[-1, 16], [-16, 8]], A.is_equal, 0.0, 0, 1), ["onf"], ["psf"])
     gc(128, lambda: sel(T.pqf[:], T.onf[:], [[-1, 8], [-8, 16]], A.is_equal, 0.0, 0, 1), ["onf"], ["pqf"])
@@ -227,13 +228,11 @@ def build(g, T, core, topo):
 
     vg(512, lambda: tc(T.obp[:], T.ob[:, 0:512].indirect(T.opu[:, 0:32])), ["ob", "opu"], ["obp"])
     for c in range(4):
-        for lo, hi in ((0, 128), (128, 256), (256, 512), (512, 1024), (1024, 1280)):
-            src = (T.obp, 128 * c, "obp") if hi <= 256 else (T.ora, 1280 * c, "ora%d" % c)
-            v(hi - lo, (lambda c=c, lo=lo, hi=hi, src=src: tc(T.ora[:, 1280 * c + lo:1280 * c + hi], src[0][:, src[1]:src[1] + hi - lo])),
-              ["obp"] + ([src[2]] if hi > 256 else []), ["ora%d" % c], half=True)
-        for r in range(2):
-            o = 256 * (c % 2) + 128 * r
-            v(128, (lambda c=c, o=o: tc(T["ox%d" % (c // 2)][:, o:o + 128], T.obp[:, 128 * c:128 * c + 128])), ["obp"], ["ox%d%d" % (c, r)])
+        for lo, hi in ((0, 128), (128, 256), (256, 512), (512, 1024)):
+            src = (T.obp, 128 * c) if hi <= 256 else (T.ora, 1024 * c)
+            v(hi - lo, (lambda c=c, lo=lo, hi=hi, src=src: tc(T.ora[:, 1024 * c + lo:1024 * c + hi], src[0][:, src[1]:src[1] + hi - lo])),
+              ["obp"] + (["ora%d" % c] if hi > 256 else []), ["ora%d" % c], half=True)
+        s(1024, (lambda c=c: act(T.nra[:, 1024 * c:1024 * c + 1024], T.ora[:, 1024 * c:1024 * c + 1024], F.Copy, scale=-1.0)), ["ora%d" % c], ["nra%d" % c])
 
     def rrs(t, ch):
         return T.rr[:, t * 512 + ch * 128:t * 512 + ch * 128 + 128]
@@ -303,9 +302,9 @@ def build(g, T, core, topo):
         fns = []
         for e in range(2):
             ch = 2 * h + e
-            fns += [mm(T.ma[:, e, :], LG[c][:, ch * 128:ch * 128 + 128], T.wq[:], True, False), mm(T.ma[:, e, :], rrs(0, ch), T.bo[:], False, True)]
-        pe(512, fns, ["lg%d%d" % (c, h), "wq", "bo"] + R0, (), ["ma"])
-        s(256, lambda: act(T.qa[:, c], T.ma[:, 0:2, :], F.Abs, bias=-127.5), (), ["qa%d" % c], ["ma"])
+            fns += [mm(T.mc[:, e, :], LG[c][:, ch * 128:ch * 128 + 128], T.wq[:], True, False), mm(T.mc[:, e, :], rrs(0, ch), T.bo[:], False, True)]
+        pe(512, fns, ["lg%d%d" % (c, h), "wq", "bo"] + R0, (), ["mc"])
+        s(256, lambda: act(T.qa[:, c], T.mc[:, 0:2, :], F.Abs, bias=-127.5), (), ["qa%d" % c], ["mc"])
         v(256, lambda: ts(T.pen[:, c, 2 * h:2 * h + 2, :], T.qa[:, c], 127.5, BIG, A.is_gt, A.mult), ["qa%d" % c], ["pen%d%d" % (c, h)], half=True)
 
     def dld(t, c, h):
@@ -335,24 +334,28 @@ def build(g, T, core, topo):
     def score(t, c, ch):
         h, e = ch // 2, ch % 2
         i = 2 * c + h
-        b, kn = 3840 * (nscore[0] % NB), "kp%d" % (nscore[0] % 3)
+        nb, kn = nscore[0] % NB, "kp%d" % (nscore[0] % NKP)
+        b = 3840 * nb
         nscore[0] += 1
         key, c0, WIN = T[kn][:, 0:128], 480 * i + 240 * e, T.pw[:, 0:8192]
         for p, ka, kb in BLOCKS:
             n = 256 * (kb - ka)
             off = T.uu[:, c0 + 16 * ka:c0 + 16 * kb]
-            o, sk, mk = T.sa[:, b + 256 * ka:b + 256 * kb], "sa%d_%d" % (b, ka), "me%d_%d" % (b, ka)
+            o, mo, sk, mk = T.sa[:, b + 256 * ka:b + 256 * kb], T.me[:, b + 256 * ka:b + 256 * kb], "sa%d_%d" % (b, ka), "me%d_%d" % (b, ka)
+            if p == "E":
+                sgt(n, (lambda o=o, off=off: act(o, WIN.indirect(off), F.Copy)), PW + ["uu%d" % i], [sk])
+                op("g", EO, [lambda o=o, n=n: g.dma_start(o, T.nra[:, 1024 * ch:1024 * ch + n], accum_op=A.add)], [sk, "nra%d" % ch], [sk],
+                   sem="e%d_%d" % (nb, ka), inc=16, lat=EL)
+            else:
+                vg(n, (lambda o=o, off=off, n=n: tt(o, WIN.indirect(off), T.ora[:, 1024 * ch:1024 * ch + n], A.subtract)), PW + ["uu%d" % i, "ora%d" % ch], [sk])
             if p == "A":
-                vg(n, (lambda o=o, off=off, n=n: tt(o, WIN.indirect(off), T.ora[:, 1280 * ch:1280 * ch + n], A.subtract)), PW + ["uu%d" % i, "ora%d" % ch], [sk])
                 s(n, (lambda o=o: act(o, o, F.Abs)), [sk], [sk])
             else:
-                sgt(n, (lambda o=o, off=off: act(o, WIN.indirect(off), F.Copy)), PW + ["uu%d" % i], [sk])
-                v(256, [(lambda x=b + 256 * x: tt(T.me[:, x:x + 256], T.sa[:, x:x + 256], T["ox%d" % h][:, 256 * e:256 * e + 256], A.max)) for x in range(ka, kb)],
-                  [sk, "ox%d0" % ch, "ox%d1" % ch], [mk])
-        pe(512, [mm(key, T.pqb[:], T.pen[:, c, ch, :], True, False), mm(key, T.one[0:1, 0:128], T.ci[0:1, 128 * c:128 * c + 128], False, False),
-                 mm(key, T.obp[:, 128 * ch:128 * ch + 128], T.box[:], False, False), mm(key, T.dm[:, 128 * ch:128 * ch + 128], T.bo32[:], False, False)],
-           ["pqb", "pen%d%d" % (c, h), "one", "ci", "obp", "box", "dm", "bo32"], (), [kn])
-        jobs = [(p, ka, kb, "a" if p == "A" else "n") for p, ka, kb in BLOCKS] + [(p, ka, kb, "m") for p, ka, kb in BLOCKS if p == "D"]
+                v(n, (lambda o=o, mo=mo: ts(mo, o, 0.0, None, A.max)), [sk], [mk], half=True)
+        pe(384, [mm(key, T.pqb[:], T.pen[:, c, ch, :], True, False), mm(key, T.one[0:1, 0:128], T.ci[0:1, 128 * c:128 * c + 128], False, False),
+                 mm(key, T.dm[:, 128 * ch:128 * ch + 128], T.bo32[:], False, False)],
+           ["pqb", "pen%d%d" % (c, h), "one", "ci", "dm", "bo32"], (), [kn])
+        jobs = [(p, ka, kb, "a" if p == "A" else "n") for p, ka, kb in BLOCKS] + [(p, ka, kb, "m") for p, ka, kb in BLOCKS if p != "A"]
         for z, (p, ka, kb, nm) in enumerate(jobs):
             buf, bk = (T.me, "me") if nm == "m" else (T.sa, "sa")
             ks = [(k, kd) for k in range(ka, kb) for kd in range(2)]
@@ -399,7 +402,7 @@ def build(g, T, core, topo):
         v(64, lambda: tt(T.e2[:], T.e1[:], T.ac[:], A.mult), ["e1"] + acs, ["e2"])
         v(64, lambda: tt(T.nx[:, n], T.e2[:], T.n1s[:], A.add), ["e2", "n1s"], ["nx%d" % (t + 1)])
         if t < RO - 1:
-            vg(512, lambda: tt(T.xx[:], T.nx[:, n].indirect(LB), T.ms[:], A.mult), ["nx%d" % (t + 1), "lb", "ms"], ["xx"])
+            vg(512, lambda: tt(T.xx[:], T.nx[:, n].indirect(LB), T.ms[:], A.mult), ["nx%d" % (t + 1), "lb", "ms", "pp"], ["xx"])
             pe(1024, [mm(T.mb[:, 1, 8 * c:8 * c + 8], T.xx[:, 128 * c:128 * c + 128], T.c8s[:], True, True) for c in range(4)], ["xx", "c8s"], (), ["mb"])
             v(32, lambda: tc(T.tn[:, 32 * t + 32:32 * t + 64], T.mb[:, 1, 0:32]), (), ["tn%d" % (t + 1)], ["mb"])
             v(64, lambda: tt(T.h1[:], T.nn[:], T.sr[:, o], A.subtract), ["nn", "sr%d" % t], ["h1"])
@@ -481,6 +484,7 @@ def schedule(ops):
     prio = [0.0] * n
     for i in range(n - 1, -1, -1):
         prio[i] = ops[i]["dur"] + ops[i]["lat"] + max([prio[j] for j in succ[i]], default=0.0)
+    prio = [p - ALPHA * i / n for i, p in enumerate(prio)]
     left = [len(o["deps"] | o["soft"]) for o in ops]
     fin, ready, free, busy = [0.0] * n, [0.0] * n, {}, {}
     avail = [i for i in range(n) if left[i] == 0]

from concourse.mybir import AluOpType, ActivationFunctionType
A = AluOpType
F = ActivationFunctionType
NK = 15
BLOCKS = [("E", 0, 4), ("E", 4, 8), ("A", 8, 12), ("B", 12, 15)]
RO = 3
BIG = float(2 ** 21)
NB, NKP = 3, 4
CY, GR, PC, EO, EL = 0.00083 * 1.15, 1.5, 0.00042 * 1.15, 1.0, 3.0
ALPHA = 150.0

SCRATCH = {}


def _decl(names, shape, dtype, where="sbuf"):
    for nm in names.split():
        SCRATCH[nm] = (where, list(shape), dtype)


_decl("pw", [128, 8192], "bfloat16")
_decl("r32 mi", [128, 512], "int32")
_decl("n32 s32 lbi opi opj ki bi cb wi wj", [128, 32], "int32")
_decl("f32i", [8, 512], "int32")
_decl("ff on8 of8", [8, 512], "float32")
_decl("ob lg0 lg1 sg eh el obp dm", [128, 512], "bfloat16")
_decl("en xx mq ms yrb k0 kd", [128, 512], "float32")
_decl("pp", [128, 4, 128], "bfloat16")
_decl("ora nra", [128, 4 * 1024], "bfloat16")
_decl("lb opu um n1t", [128, 32], "uint16")
_decl("zm uim", [128, 8, 4], "int32")
_decl("tt kb m01 onf idf psf pqf", [128, 128], "float32")
_decl("t8", [128, 64], "float32")
_decl("t4 kk n1q n1s dn a1 nn wv e1 e2 g1 h1 l2 th hit nf", [128, 32], "float32")
_decl("t2", [128, 16], "float32")
_decl("ac", [128, 32], "bfloat16")
_decl("oh", [128, 1024], "bfloat16")
_decl("oha", [128, 2, 128], "bfloat16")
_decl("dd", [128, 4, 4, 128], "bfloat16")
_decl("x2", [128, 4, 8, 16], "bfloat16")
_decl("an a8", [128, 8], "int32")
_decl("qi", [128, 96], "float32")
_decl("one", [128, 248], "bfloat16")
_decl("g8f c8s", [128, 8], "float32")
_decl("g8b g8h w0 w1 wsw", [128, 8], "bfloat16")
_decl("bo nbo bo32 idb nid wq psb pqb", [128, 128], "bfloat16")
_decl("bw tga tha tgn thn tgm thm", [128, 8, 31], "bfloat16")
_decl("wt", [128, 8, 15], "bfloat16")
_decl("wgh wb", [128, 8, 15, 2], "bfloat16")
_decl("wh wl", [128, 8, 16], "bfloat16")
_decl("ci", [1, 256], "bfloat16")
_decl("odd", [128, 4], "float32")
_decl("sa me", [128, NB * 3840], "bfloat16")
_decl("zi", [128, 4, 8, 2, 30], "int32")
_decl("ui", [128, 4, 8, 60], "int32")
_decl("uu", [128, 4 * 480], "uint16")
_decl("qa", [128, 2, 2, 128], "bfloat16")
_decl("pen", [128, 2, 4, 128], "bfloat16")
_decl("rr lw sw so", [128, RO * 512], "bfloat16")
_decl("tn", [128, RO * 32], "uint16")
_decl("nx sr fx", [128, 4 * 32], "float32")
_decl("kp0 kp1 kp2 kp3", [128, 512], "float32", "psum")
_decl("px", [128, 2, 8, 32], "float32", "psum")
_decl("ma mb mc", [128, 4, 128], "float32", "psum")

PARTS = [(0, 256), (256, 384), (384, 512)]
SEMAPHORES = ["qv", "qs", "qp", "qg", "ldr", "ldn", "ldo", "lds", "ldf", "ldp", "ldq", "ixm", "ls", "oy", "oz", "on", "of"]
SEMAPHORES += ["ix%d" % i for i in range(4)] + ["al0"] + ["al%d%d" % (t, p) for t in (1, 2) for p in range(3)] + ["as%d" % t for t in range(3)]
SEMAPHORES += ["e%d_%d" % (b, ka) for b in range(NB) for p, ka, kb in BLOCKS if p == "E"]


def build(g, T, core, topo):
    ops = []
    lastw, readers, bank = {}, {}, {}

    def op(q, dur, fns, r=(), w=(), banks=(), sem=None, inc=0, lat=0.0, deps=()):
        i = len(ops)
        dp, soft = set(deps), set()
        for k in r:
            if k not in lastw:
                raise ValueError("read before write " + k)
            dp.add(lastw[k])
        for k in w:
            if k in lastw:
                dp.add(lastw[k])
            dp.update(readers.get(k, ()))
        for k in r:
            readers.setdefault(k, set()).add(i)
        for k in w:
            lastw[k] = i
            readers[k] = set()
        for b in banks:
            st = bank.setdefault(b, {"e": None, "cur": [], "prev": []})
            if st["e"] != q:
                st["prev"], st["cur"], st["e"] = st["cur"], [], q
            elif q == "p" and st["cur"]:
                soft.add(st["cur"][-1])
            dp.update(st["prev"])
            st["cur"].append(i)
        dp.discard(i)
        ops.append({"q": q, "dur": dur, "fns": fns, "deps": dp, "soft": soft - dp, "sem": sem, "inc": inc, "lat": lat, "remote": False})
        return i

    def v(n, fn, r=(), w=(), banks=(), half=False):
        fns = fn if isinstance(fn, list) else [fn]
        return op("v", len(fns) * max(64, n * (0.5 if half else 1)) * CY, fns, r, w, banks)

    def vg(n, fn, r=(), w=()):
        return op("v", 0.05 + n * GR * CY, [fn], r, w)

    def s(n, fn, r=(), w=(), banks=()):
        fns = fn if isinstance(fn, list) else [fn]
        return op("s", len(fns) * (0.03 + n * CY), fns, r, w, banks)

    def sgt(n, fn, r=(), w=()):
        return op("s", 0.065 + n * GR * CY, [fn], r, w)

    def mm(out, lhsT, rhs, st, sp):
        return lambda: g.tensor.matmul(out, lhsT, rhs, st, sp)

    def pe(cyc, fns, r=(), w=(), banks=()):
        return op("p", cyc * PC, fns, r, w, banks)

    def gc(n, fn, r=(), w=()):
        return op("g", 0.17 + 2 * n * CY, [fn], r, w)

    tt, ts, tc, fill = g.vector.tensor_tensor, g.vector.tensor_scalar, g.vector.tensor_copy, g.vector.memset
    act, sel = g.scalar.activation, g.affine_select
    rank = T.rank_of(core)

    def send(t, dst_t, src, sem_name, r, name):
        p = T.cores[(rank - 1 - t % 7) % 8]
        rid, pid, _ = topo.addr(p)
        mask = 0
        for e in topo.engines(core, p)[:8]:
            mask |= 1 << e
        i = op("g", 1.0, [lambda: g.remote_dma(dst_t, src, T.sem[sem_name], T.sem.ls, pid, rid, mask)], r, (), sem="ls", inc=8, lat=2.0)
        ops[i]["remote"] = True
        return op(None, 0.0, [], (), [name], deps=(i,), sem=sem_name, inc=8, lat=0.3)

    def load(q, out, in_, sem, key, lat):
        eng = g.sync if q == "y" else g.scalar
        return op(q, 0.1, [lambda: eng.dma_start(out, in_)], (), [key], sem=sem, inc=16, lat=lat)
    load("y", T.r32[:], T.resid[:], "ldr", "r32", 3.0)
    load("s", T.n32[:], T.nx0[:], "ldn", "n32", 2.5)
    load("s", T.s32[:], T.src0[:], "lds", "s32", 2.5)
    load("s", T.ob[:], T.obs[:], "ldo", "ob", 3.0)
    load("s", T.f32i[:], T.fit0[:], "ldf", "f32i", 3.0)
    load("y", T.pw[:, 0:4096], T.prof[:, 0:4096], "ldp", "pw0", 8.0)
    load("y", T.pw[:, 4096:8192], T.prof[:, 4096:8192], "ldq", "pw1", 11.0)
    PW = ["pw0", "pw1"]
    v(248, lambda: fill(T.one[:], 1.0), (), ["one"])
    v(128, lambda: fill(T.onf[:], 1.0), (), ["onf"])
    gc(120, lambda: sel(T.wt[:], T.one[:, 0:120], [[-16, 8], [0, 15]], A.is_ge, 0.0, 0, 1), ["one"], ["wtA"])
    gc(120, lambda: sel(T.wt[:], T.wt[:], [[16, 8], [0, 15]], A.is_ge, 0.0, 15, -1), ["wtA"], ["wtB"])
    v(120, lambda: tc(T.wb[:, :, :, 1], T.wt[:]), ["wtB"], ["wb1"])
    v(120, lambda: fill(T.wb[:, :, :, 0], 0.0), (), ["wb0"])
    gc(120, lambda: sel(T.wt[:], T.wt[:], [[16, 8], [1, 15]], A.is_ge, 0.0, 0, -1), ["wtB"], ["wtB", "wt"])
    v(120, lambda: tc(T.wgh[:, :, :, 0], T.wt[:]), ["wt"], ["wgh0"])
    v(240, lambda: tt(T.wgh[:, :, :, 1], T.wt[:], T.wb[:, :, :, 1], A.subtract), ["wt", "wb1"], ["wgh1"])
    WGH, WB = ["wgh0", "wgh1"], ["wb0", "wb1"]
    gc(4, lambda: g.iota(T.odd[:], [[256, 4]], 1, 2, allow_small_or_imprecise_dtypes=True), (), ["odd"])
    gc(32, lambda: g.iota(T.lbi[:], [[1, 32]], 0, 0), (), ["lbi"])
    v(32, lambda: tc(T.lb[:], T.lbi[:]), ["lbi"], ["lb"])
    gc(512, lambda: g.iota(T.mi[:], [[0, 32], [-1, 16]], 0, 1), (), ["mi"])
    v(512, lambda: ts(T.mi[:], T.mi[:], 15, None, A.bitwise_and), ["mi"], ["mi"])
    v(512, lambda: ts(T.mq[:], T.mi[:], 0.0, None, A.is_equal), ["mi"], ["mq"])
    gc(32, lambda: g.iota(T.opi[:], [[0, 4], [1, 8]], 0, 8), (), ["opi"])
    gc(32, lambda: g.iota(T.opj[:], [[128, 4], [0, 8]], 0, 0), (), ["opj"])
    v(32, lambda: ts(T.opi[:], T.opi[:], 127, None, A.bitwise_and), ["opi"], ["opi"])
    v(64, lambda: tt(T.opj[:], T.opi[:], T.opj[:], A.add), ["opi", "opj"], ["opj"])
    v(32, lambda: tc(T.opu[:], T.opj[:]), ["opj"], ["opu"])
    gc(128, lambda: sel(T.bo[:], T.one[:, 0:128], [[-16, 8], [0, 16]], A.is_ge, 0.0, 0, 1), ["one"], ["bo_"])
    gc(128, lambda: sel(T.bo[:], T.bo[:], [[16, 8], [0, 16]], A.is_ge, 0.0, 15, -1), ["bo_"], ["bo_", "bo"])
    gc(8, lambda: sel(T.g8f[:], T.onf[:, 0:8], [[-16, 8]], A.is_ge, 0.0, 0, 1), ["onf"], ["g8_"])
    gc(8, lambda: sel(T.g8f[:], T.g8f[:], [[16, 8]], A.is_ge, 0.0, 15, -1), ["g8_"], ["g8_", "g8f"])
    v(8, lambda: tc(T.g8b[:], T.g8f[:]), ["g8f"], ["g8b"])
    v(8, lambda: ts(T.g8h[:], T.g8f[:], 256.0, None, A.mult), ["g8f"], ["g8h"])
    gc(128, lambda: sel(T.idf[:], T.onf[:], [[-1, 128]], A.is_equal, 0.0, 0, 1), ["onf"], ["idf"])
    v(128, lambda: tc(T.idb[:], T.idf[:]), ["idf"], ["idb"])
    v(128, lambda: ts(T.nid[:], T.idf[:], -1.0, None, A.mult), ["idf"], ["nid"])
    v(256, lambda: tt(T.wq[:], T.idb[:], T.bo[:], A.subtract), ["idb", "bo"], ["wq"])
    for nm, f in (("nbo", -1.0), ("bo32", 32.0)):
        v(128, (lambda nm=nm, f=f: ts(T[nm][:], T.bo[:], f, None, A.mult)), ["bo"], [nm], half=True)
    gc(128, lambda: sel(T.psf[:], T.onf[:], [[-1, 16], [-16, 8]], A.is_equal, 0.0, 0, 1), ["onf"], ["psf"])
    gc(128, lambda: sel(T.pqf[:], T.onf[:], [[-1, 8], [-8, 16]], A.is_equal, 0.0, 0, 1), ["onf"], ["pqf"])
    v(128, lambda: tc(T.psb[:], T.psf[:]), ["psf"], ["psb"])
    v(128, lambda: tc(T.pqb[:], T.pqf[:]), ["pqf"], ["pqb"])
    gc(8, lambda: sel(T.w0[:], T.one[:, 0:8], [[-16, 8]], A.is_equal, 0.0, 0, 1), ["one"], ["w0"])
    gc(8, lambda: sel(T.w1[:], T.one[:, 0:8], [[-16, 8]], A.is_equal, 0.0, -1, 1), ["one"], ["w1"])
    v(8, lambda: ts(T.w0[:], T.w0[:], 256.0, None, A.mult), ["w0"], ["w0"])
    v(16, lambda: tt(T.wsw[:], T.w0[:], T.w1[:], A.add), ["w0", "w1"], ["wsw"])
    for x, nm in enumerate(("wh", "wl")):
        v(128, (lambda nm=nm: fill(T[nm][:], 0.0)), (), [nm])
        v(8, (lambda nm=nm, x=x: tc(T[nm][:, :, x], T.g8f[:])), ["g8f"], [nm])
    gc(256, lambda: g.iota(T.ci[:], [[16, 2], [0, 8], [1, 16]], 32, 0, allow_small_or_imprecise_dtypes=True), (), ["ci"])
    gc(248, lambda: sel(T.bw[:], T.one[:], [[-16, 8], [0, 31]], A.is_ge, 0.0, 0, 1), ["one"], ["bw_"])
    gc(248, lambda: sel(T.bw[:], T.bw[:], [[16, 8], [0, 31]], A.is_ge, 0.0, 15, -1), ["bw_"], ["bw_", "bw"])
    TK = {}
    for nm, f in (("a", 32.0), ("n", -32.0), ("m", 64.0)):
        TK[nm] = []
        for tx, lo, hi in (("tg", 0.0, f), ("th", f, 0.0)):
            for a, b, c in ((0, 15, lo), (15, 31, hi)):
                v(8 * (b - a), (lambda tx=tx, nm=nm, a=a, b=b, c=c: ts(T[tx + nm][:, :, a:b], T.bw[:, :, a:b], c, None, A.mult)), ["bw"], [tx + nm + str(a)], half=True)
                TK[nm].append(tx + nm + str(a))
    v(128, lambda: fill(T.m01[:], 1.0), (), ["m01"])
    v(8, lambda: fill(T.m01[:, 0:128:16], 0.0), (), ["m01"])
    v(512, lambda: fill(T.kd[:], 0.0), (), ["kd%d" % c for c in range(4)])
    v(512, lambda: fill(T.x2[:], 0.0), (), ["x2h", "x2l"])
    v(8, lambda: fill(T.an[:], 0), (), ["an"])

    v(512, lambda: tc(T.rr[:, 0:512], T.r32[:]), ["r32"], ["rr0_%d" % c for c in range(4)])
    R0 = ["rr0_%d" % c for c in range(4)]
    v(32, lambda: tc(T.tn[:, 0:32], T.n32[:]), ["n32"], ["tn0"])
    send(0, T.lw[:, 0:512], T.rr[:, 0:512], "al0", R0, "lw0_0")
    v(32, lambda: ts(T.hit[:], T.s32[:], 256.0, None, A.is_ge), ["s32"], ["hit"])
    v(32, lambda: ts(T.l2[:], T.hit[:], -256.0, None, A.mult), ["hit"], ["l2"])
    v(64, lambda: tt(T.l2[:], T.l2[:], T.s32[:], A.add), ["l2", "s32"], ["l2"])
    LB = T.lb[:, 0:32]
    vg(512, lambda: tt(T.eh[:], T.hit[:, 0:32].indirect(LB), T.mq[:], A.mult), ["hit", "lb", "mq"], ["eh"])
    vg(512, lambda: tt(T.el[:], T.l2[:, 0:32].indirect(LB), T.mq[:], A.mult), ["l2", "lb", "mq"], ["el"])
    pe(1024, [f for c in range(4) for f in (mm(T.mb[:, c, :], T.wh[:], T.eh[:, 128 * c:128 * c + 128], True, False),
                                            mm(T.mb[:, c, :], T.wl[:], T.el[:, 128 * c:128 * c + 128], False, True))], ["wh", "wl", "eh", "el"], (), ["mb"])

    def copy4(dst, o, key, bk="mb", rows=128):
        s(128, [(lambda c=c: act(dst[0:rows, o + 128 * c:o + 128 * c + 128], T[bk][0:rows, c, :], F.Copy)) for c in range(4)], (), [key], [bk])
    copy4(T.so, 0, "so0")
    send(0, T.sw[:, 0:512], T.so[:, 0:512], "as0", ["so0"], "sw0")

    vg(512, lambda: tc(T.obp[:], T.ob[:, 0:512].indirect(T.opu[:, 0:32])), ["ob", "opu"], ["obp"])
    for c in range(4):
        for lo, hi in ((0, 128), (128, 256), (256, 512), (512, 1024)):
            src = (T.obp, 128 * c) if hi <= 256 else (T.ora, 1024 * c)
            v(hi - lo, (lambda c=c, lo=lo, hi=hi, src=src: tc(T.ora[:, 1024 * c + lo:1024 * c + hi], src[0][:, src[1]:src[1] + hi - lo])),
              ["obp"] + (["ora%d" % c] if hi > 256 else []), ["ora%d" % c], half=True)
        s(1024, (lambda c=c: act(T.nra[:, 1024 * c:1024 * c + 1024], T.ora[:, 1024 * c:1024 * c + 1024], F.Copy, scale=-1.0)), ["ora%d" % c], ["nra%d" % c])

    def rrs(t, ch):
        return T.rr[:, t * 512 + ch * 128:t * 512 + ch * 128 + 128]

    def own_mass():
        pe(256, [mm(T.ma[:, 0, 8 * c:8 * c + 8], rrs(0, c), T.g8b[:], True, True) for c in range(4)], R0 + ["g8b"], (), ["ma"])
        v(8, [(lambda c=c: ts(T.zm[:, :, c], T.ma[:, 0, 8 * c:8 * c + 8], 4096.0, T.odd[:, c:c + 1], A.add, A.mult)) for c in range(4)], ["odd"], ["zm"], ["ma"])
        v(32, lambda: ts(T.zm[:], T.zm[:], 1, 8191, A.arith_shift_right, A.bitwise_and), ["zm"], ["zm"])
        op("y", 0.6, [(lambda k=k: g.sync.dma_start(T.uim[16 * k:16 * k + 16, :, :], T.zm[:, k, :])) for k in range(8)], ["zm"], ["uim"], sem="ixm", inc=128, lat=2.5)
        v(4, [(lambda b=b: tc(T.um[:, b:32:8], T.uim[:, b, :])) for b in range(8)], ["uim"], ["um"])
        vg(512, lambda: tt(T.dm[:], T.pw[:, 0:8192].indirect(T.um[:, 0:32]), T.obp[:], A.subtract), PW + ["um", "obp"], ["dm"])
        s(512, lambda: act(T.dm[:], T.dm[:], F.Abs), ["dm"], ["dm"])

    def init_scalars():
        v(32, lambda: tc(T.nf[:], T.n32[:]), ["n32"], ["nf"])
        vg(512, lambda: tt(T.en[:], T.nf[:, 0:32].indirect(LB), T.mq[:], A.mult), ["nf", "lb", "mq"], ["en"])
        op("v", 512 * CY, [lambda: tc(T.ff[:], T.f32i[:])], ["f32i"], ["ff"])
        fns = []
        for c in range(4):
            sl = slice(c * 128, c * 128 + 128)
            fns += [mm(T.mb[:, 0, 8 * c:8 * c + 8], T.en[:, sl], T.g8f[:], True, True),
                    mm(T.mb[:, 0, 32 + 8 * c:40 + 8 * c], T.eh[:, sl], T.g8h[:], True, False),
                    mm(T.mb[:, 0, 32 + 8 * c:40 + 8 * c], T.el[:, sl], T.g8b[:], False, True),
                    mm(T.mb[:, 0, 64 + 8 * c:72 + 8 * c], T.ff[0:8, sl], T.idf[0:8, 0:8], True, True)]
        pe(40 * 64, fns, ["en", "eh", "el", "ff", "g8f", "g8b", "g8h", "idf"], (), ["mb"])
        v(96, lambda: tc(T.qi[:], T.mb[:, 0, 0:96]), (), ["qi"], ["mb"])
        pe(512, [mm(T.mb[:, 1, 0:96], T.pqf[:], T.qi[:], True, True)], ["pqf", "qi"], (), ["mb"])
        v(32, lambda: tc(T.nx[:, 0:32], T.mb[:, 1, 0:32]), (), ["nx0"], ["mb"])
        v(32, lambda: tc(T.sr[:, 0:32], T.mb[:, 1, 32:64]), (), ["sr0"], ["mb"])
        v(32, lambda: ts(T.fx[:, 0:32], T.mb[:, 1, 64:96], 1.0, None, A.add), (), ["fx0"], ["mb"])
        v(32, lambda: ts(T.th[:], T.fx[:, 0:32], 32.0, None, A.mult), ["fx0"], ["th"])
        pe(2048 + 256, [mm(T.mb[:, c, :], T.pqf[:], T.mq[:, 128 * c:128 * c + 128], True, True) for c in range(4)], ["pqf", "mq"], (), ["mb"])
        copy4(T.ms, 0, "ms")
        pe(256, [mm(T.mb[:, 0, 0:8], T.pqf[:], T.g8f[:], True, True)], ["pqf", "g8f"], (), ["mb"])
        v(8, lambda: tc(T.c8s[:], T.mb[:, 0, 0:8]), (), ["c8s"], ["mb"])

    LG = [T.lg0, T.lg1]
    nscore = [0]

    def gather_lists(t, c):
        tk = "tn%d" % t if c == 0 else "n1t"
        win = T.lw[:, 512 * t:512 * t + 512]
        lws = ["lw%d_%d" % (t, p) for p in range(1 if t == 0 else 3)]
        for h in range(2):
            idx = T.tn[:, 32 * t + 16 * h:32 * t + 16 * h + 16] if c == 0 else T.n1t[:, 16 * h:16 * h + 16]
            o = LG[c][:, 256 * h:256 * h + 256]
            if h == 0 and c == 0:
                vg(256, (lambda o=o, idx=idx: tc(o, win.indirect(idx))), lws + [tk], ["lg%d%d" % (c, h)])
            else:
                sgt(256, (lambda o=o, idx=idx: act(o, win.indirect(idx), F.Copy)), lws + [tk], ["lg%d%d" % (c, h)])

    def index(t, c, h):
        lk, i = "lg%d%d" % (c, h), 2 * c + h
        zk = "zi%d" % i
        fns = []
        for e in range(2):
            ch = 2 * h + e
            fns += [mm(T.px[:, e, :, 0:30], LG[c][:, ch * 128:ch * 128 + 128], T.wgh[:], True, False),
                    mm(T.px[:, e, :, 0:30], rrs(0, ch), T.wb[:], False, True)]
        pe(960, fns, [lk] + WGH + WB + R0, (), ["px"])
        v(240, [(lambda e=e: ts(T.zi[:, i, :, e, :], T.px[:, e, :, 0:30], 4096.0, T.odd[:, 2 * h + e:2 * h + e + 1], A.add, A.mult)) for e in range(2)], ["odd"], [zk], ["px"])
        v(480, lambda: ts(T.zi[:, i], T.zi[:, i], 1, 8191, A.arith_shift_right, A.bitwise_and), [zk], [zk])
        op("y", 0.6, [(lambda k=k: g.sync.dma_start(T.ui[16 * k:16 * k + 16, i, :, :], T.zi[:, i, k, :, :])) for k in range(8)], [zk], ["ui%d" % i], sem="ix%d" % i, inc=128, lat=3.0)
        v(60, [(lambda b=b: tc(T.uu[:, 480 * i + b:480 * i + 480:8], T.ui[:, i, b, :])) for b in range(8)], ["ui%d" % i], ["uu%d" % i])

    def pen(t, c, h):
        fns = []
        for e in range(2):
            ch = 2 * h + e
            fns += [mm(T.mc[:, e, :], LG[c][:, ch * 128:ch * 128 + 128], T.wq[:], True, False), mm(T.mc[:, e, :], rrs(0, ch), T.bo[:], False, True)]
        pe(512, fns, ["lg%d%d" % (c, h), "wq", "bo"] + R0, (), ["mc"])
        s(256, lambda: act(T.qa[:, c], T.mc[:, 0:2, :], F.Abs, bias=-127.5), (), ["qa%d" % c], ["mc"])
        v(256, lambda: ts(T.pen[:, c, 2 * h:2 * h + 2, :], T.qa[:, c], 127.5, BIG, A.is_gt, A.mult), ["qa%d" % c], ["pen%d%d" % (c, h)], half=True)

    def dld(t, c, h):
        hs = slice(256 * h, 256 * h + 256)
        rk = ["rr%d_%d" % (t, 2 * h), "rr%d_%d" % (t, 2 * h + 1)]
        rt = T.rr[:, t * 512 + 256 * h:t * 512 + 256 * h + 256]
        pe(1024, [mm(T.ma[:, 0:2, :], T.idb[:], LG[c][:, hs], True, False), mm(T.ma[:, 0:2, :], T.nid[:], rt, False, True),
                  mm(T.ma[:, 2:4, :], T.nbo[:], LG[c][:, hs], True, False), mm(T.ma[:, 2:4, :], T.bo[:], T.rr[:, hs], False, True)],
           ["lg%d%d" % (c, h), "idb", "nid", "nbo", "bo"] + rk + R0, (), ["ma"])
        for x in range(2):
            s(256, (lambda x=x: act(T.dd[:, 2 * h:2 * h + 2, 2 * x + c, :], T.ma[:, 2 * x:2 * x + 2, :], F.Copy)), (), ["dd%d%d%d" % (c, h, x)], ["ma"])

    def n1_chain(t):
        sgt(512, lambda: act(T.sg[:], T.sw[:, 512 * t:512 * t + 512].indirect(T.tn[:, 32 * t:32 * t + 32]), F.Copy), ["sw%d" % t, "tn%d" % t], ["sg"])
        pe(256, [mm(T.ma[:, 0, 8 * c:8 * c + 8], T.sg[:, 128 * c:128 * c + 128], T.wsw[:], True, True) for c in range(4)], ["sg", "wsw"], (), ["ma"])
        v(32, lambda: tc(T.n1q[:], T.ma[:, 0, 0:32]), (), ["n1q"], ["ma"])
        vg(512, lambda: tt(T.xx[:], T.n1q[:, 0:32].indirect(LB), T.mq[:], A.mult), ["n1q", "lb", "mq"], ["xx"])
        pe(1280, [mm(T.ma[:, 1, 8 * c:8 * c + 8], T.xx[:, 128 * c:128 * c + 128], T.g8f[:], True, True) for c in range(4)] +
           [mm(T.ma[:, 1, 32:64], T.pqf[:], T.n1q[:], True, True)], ["xx", "g8f", "pqf", "n1q"], (), ["ma"])
        v(32, lambda: tc(T.n1t[:], T.ma[:, 1, 0:32]), (), ["n1t"], ["ma"])
        v(32, lambda: tc(T.n1s[:], T.ma[:, 1, 32:64]), (), ["n1s"], ["ma"])
        v(64, lambda: tt(T.dn[:], T.n1s[:], T.nx[:, 32 * t:32 * t + 32], A.subtract), ["n1s", "nx%d" % t], ["dn"])

    def wsl(nm, kd, k):
        return T[("th" if kd else "tg") + nm][:, :, 14 - k:30 - k]

    def score(t, c, ch):
        h, e = ch // 2, ch % 2
        i = 2 * c + h
        nb, kn = nscore[0] % NB, "kp%d" % (nscore[0] % NKP)
        b = 3840 * nb
        nscore[0] += 1
        key, c0, WIN = T[kn][:, 0:128], 480 * i + 240 * e, T.pw[:, 0:8192]
        for p, ka, kb in BLOCKS:
            n = 256 * (kb - ka)
            off = T.uu[:, c0 + 16 * ka:c0 + 16 * kb]
            o, mo, sk, mk = T.sa[:, b + 256 * ka:b + 256 * kb], T.me[:, b + 256 * ka:b + 256 * kb], "sa%d_%d" % (b, ka), "me%d_%d" % (b, ka)
            if p == "E":
                sgt(n, (lambda o=o, off=off: act(o, WIN.indirect(off), F.Copy)), PW + ["uu%d" % i], [sk])
                op("g", EO, [lambda o=o, n=n: g.dma_start(o, T.nra[:, 1024 * ch:1024 * ch + n], accum_op=A.add)], [sk, "nra%d" % ch], [sk],
                   sem="e%d_%d" % (nb, ka), inc=16, lat=EL)
            else:
                vg(n, (lambda o=o, off=off, n=n: tt(o, WIN.indirect(off), T.ora[:, 1024 * ch:1024 * ch + n], A.subtract)), PW + ["uu%d" % i, "ora%d" % ch], [sk])
            if p == "A":
                s(n, (lambda o=o: act(o, o, F.Abs)), [sk], [sk])
            else:
                v(n, (lambda o=o, mo=mo: ts(mo, o, 0.0, None, A.max)), [sk], [mk], half=True)
        pe(384, [mm(key, T.pqb[:], T.pen[:, c, ch, :], True, False), mm(key, T.one[0:1, 0:128], T.ci[0:1, 128 * c:128 * c + 128], False, False),
                 mm(key, T.dm[:, 128 * ch:128 * ch + 128], T.bo32[:], False, False)],
           ["pqb", "pen%d%d" % (c, h), "one", "ci", "dm", "bo32"], (), [kn])
        jobs = [(p, ka, kb, "a" if p == "A" else "n") for p, ka, kb in BLOCKS] + [(p, ka, kb, "m") for p, ka, kb in BLOCKS if p != "A"]
        for z, (p, ka, kb, nm) in enumerate(jobs):
            buf, bk = (T.me, "me") if nm == "m" else (T.sa, "sa")
            ks = [(k, kd) for k in range(ka, kb) for kd in range(2)]
            pe(128 * len(ks), [mm(key, buf[:, b + 256 * k + 128 * kd:b + 256 * k + 128 * kd + 128], wsl(nm, kd, k), False, z == len(jobs) - 1 and (k, kd) == ks[-1]) for k, kd in ks],
               ["%s%d_%d" % (bk, b, ka)] + TK[nm], (), [kn])
        return kn

    def tail(t, ch, kn):
        h, key, c128, k8 = ch // 2, T[kn][:, 0:128], slice(128 * ch, 128 * ch + 128), slice(8 * ch, 8 * ch + 8)
        k0, oh = T.k0[:, c128], [T.oh[:, 256 * ch + 128 * c:256 * ch + 128 * c + 128] for c in range(2)]
        v(128, lambda: tt(T.tt[:], key, k0, A.min), ["k0%d" % ch], ["tt"], [kn])
        v(128, lambda: tt(T.t8[:], T.tt[:, 0:128:2], T.tt[:, 1:128:2], A.min), ["tt"], ["t8"])
        v(64, lambda: tt(T.t4[:], T.t8[:, 0:64:2], T.t8[:, 1:64:2], A.min), ["t8"], ["t4"])
        v(32, lambda: tt(T.t2[:], T.t4[:, 0:32:2], T.t4[:, 1:32:2], A.min), ["t4"], ["t2"])
        v(16, lambda: tt(T.kk[:, k8], T.t2[:, 0:16:2], T.t2[:, 1:16:2], A.min), ["t2"], ["kk%d" % ch])
        v(16, lambda: tt(T.ac[:, k8], T.kk[:, k8], T.th[:, k8], A.is_lt), ["kk%d" % ch, "th"], ["ac%d" % ch])
        v(16, lambda: tt(T.kd[:, 128 * ch:128 * ch + 128:16], T.kk[:, k8], T.ac[:, k8], A.mult), ["kk%d" % ch, "ac%d" % ch], ["kd%d" % ch])
        v(128, lambda: g.vector.tensor_tensor_scan(T.kb[:], T.m01[:], T.kd[:, c128], 0.0, A.mult, A.add), ["m01", "kd%d" % ch], ["kb"])
        v(128, lambda: tt(oh[1], key, T.kb[:], A.is_equal), ["kb"], ["oh1%d" % ch], [kn])
        v(256, lambda: tt(oh[0], k0, T.kb[:], A.is_equal), ["kb", "k0%d" % ch], ["oh0%d" % ch])
        pe(256, [mm(T.mb[:, c, :], oh[c], T.psb[:], True, True) for c in range(2)], ["oh0%d" % ch, "oh1%d" % ch, "psb"], (), ["mb"])
        s(256, lambda: act(T.oha[:], T.mb[:, 0:2, :], F.Copy), (), ["oha"], ["mb"])
        pe(512, [mm(T.mb[:, 0:2, :], T.bo[:], T.oha[:], True, True), mm(T.mb[:, 2:4, :], T.idb[:], T.oha[:], True, True)], ["bo", "idb", "oha"], (), ["mb"])
        v(512, lambda: tt(T.pp[:], T.mb[:], T.dd[:, ch], A.mult), ["dd%d%d%d" % (c, h, x) for c in range(2) for x in range(2)], ["pp"], ["mb"])
        pe(640, [mm(T.mb[:, 0, :], T.idb[:], rrs(t, ch), True, False)] + [mm(T.mb[:, 0, :], T.idb[:], T.pp[:, x, :], False, x == 3) for x in range(4)],
           ["idb", "rr%d_%d" % (t, ch), "pp"], (), ["mb"])
        if t < RO - 1:
            s(128, lambda: act(rrs(t + 1, ch), T.mb[:, 0, :], F.Copy), (), ["rr%d_%d" % (t + 1, ch)], ["mb"])
        else:
            s(128, lambda: act(T.yrb[:, c128], T.mb[:, 0, :], F.Copy), (), ["yrb%d" % ch], ["mb"])

    def scalars(t):
        o, n = slice(32 * t, 32 * t + 32), slice(32 * t + 32, 32 * t + 64)
        kks, acs = ["kk%d" % c for c in range(4)], ["ac%d" % c for c in range(4)]
        v(32, lambda: tc(T.ki[:], T.kk[:]), kks, ["ki"])
        v(32, lambda: ts(T.cb[:], T.ki[:], 4, 1, A.arith_shift_right, A.bitwise_and), ["ki"], ["cb"])
        v(32, lambda: ts(T.bi[:], T.ki[:], 5, None, A.arith_shift_right), ["ki"], ["bi"])
        v(64, lambda: tt(T.a1[:], T.cb[:], T.dn[:], A.mult), ["cb", "dn"], ["a1"])
        v(64, lambda: tt(T.nn[:], T.a1[:], T.nx[:, o], A.add), ["a1", "nx%d" % t], ["nn"])
        v(32, lambda: ts(T.wv[:], T.nn[:], 13.0, -1.0, A.mult, A.add), ["nn"], ["wv"])
        v(64, lambda: tt(T.wi[:], T.wv[:], T.bi[:], A.add), ["wv", "bi"], ["wi"])
        v(32, lambda: ts(T.wj[:], T.wi[:], 511, None, A.bitwise_and), ["wi"], ["wj"])
        v(64, lambda: tt(T.e1[:], T.wj[:], T.n1s[:], A.subtract), ["wj", "n1s"], ["e1"])
        v(64, lambda: tt(T.e2[:], T.e1[:], T.ac[:], A.mult), ["e1"] + acs, ["e2"])
        v(64, lambda: tt(T.nx[:, n], T.e2[:], T.n1s[:], A.add), ["e2", "n1s"], ["nx%d" % (t + 1)])
        if t < RO - 1:
            vg(512, lambda: tt(T.xx[:], T.nx[:, n].indirect(LB), T.ms[:], A.mult), ["nx%d" % (t + 1), "lb", "ms", "pp"], ["xx"])
            pe(1024, [mm(T.mb[:, 1, 8 * c:8 * c + 8], T.xx[:, 128 * c:128 * c + 128], T.c8s[:], True, True) for c in range(4)], ["xx", "c8s"], (), ["mb"])
            v(32, lambda: tc(T.tn[:, 32 * t + 32:32 * t + 64], T.mb[:, 1, 0:32]), (), ["tn%d" % (t + 1)], ["mb"])
            v(64, lambda: tt(T.h1[:], T.nn[:], T.sr[:, o], A.subtract), ["nn", "sr%d" % t], ["h1"])
            v(64, lambda: tt(T.h1[:], T.h1[:], T.ac[:], A.mult), ["h1"] + acs, ["h1"])
            v(64, lambda: tt(T.sr[:, n], T.h1[:], T.sr[:, o], A.add), ["h1", "sr%d" % t], ["sr%d" % (t + 1)])
            v(32, lambda: ts(T.l2[:], T.sr[:, n], 256.0, -256.0, A.is_ge, A.mult), ["sr%d" % (t + 1)], ["l2"])
            XK = []
            for ch in range(4):
                k8, n8 = slice(8 * ch, 8 * ch + 8), slice(32 * t + 32 + 8 * ch, 32 * t + 40 + 8 * ch)
                v(8, (lambda ch=ch, n8=n8: ts(T.x2[:, ch, :, 0], T.sr[:, n8], 256.0, None, A.is_ge)), ["sr%d" % (t + 1), "x2h"], ["x2h%d" % ch])
                v(16, (lambda ch=ch, n8=n8, k8=k8: tt(T.x2[:, ch, :, 1], T.l2[:, k8], T.sr[:, n8], A.add)), ["sr%d" % (t + 1), "l2", "x2l"], ["x2l%d" % ch])
                XK += ["x2h%d" % ch, "x2l%d" % ch]
            pe(512, [mm(T.mb[:, c, :], T.x2[:, c], T.psb[:], True, True) for c in range(4)], XK + ["psb"], (), ["mb"])
            copy4(T.so, 512 * t + 512, "so%d" % (t + 1))
        v(64, lambda: tt(T.g1[:], T.bi[:], T.fx[:, o], A.subtract), ["bi", "fx%d" % t], ["g1"])
        v(64, lambda: tt(T.g1[:], T.g1[:], T.ac[:], A.mult), ["g1"] + acs, ["g1"])
        v(64, lambda: tt(T.fx[:, n], T.g1[:], T.fx[:, o], A.add), ["g1", "fx%d" % t], ["fx%d" % (t + 1)])

    def thresholds(t):
        n = 32 * t + 32
        acs = ["ac%d" % c for c in range(4)]
        pe(256, [mm(T.ma[:, 0, 0:8], T.one[:, 0:128], T.ac[:, 8 * c:8 * c + 8], c == 0, c == 3) for c in range(4)], ["one"] + acs, (), ["ma"])
        v(16, lambda: tt(T.an[:], T.ma[:, 0, 0:8], T.an[:], A.add), ["an"], ["an"], ["ma"])
        v(8, lambda: ts(T.a8[:], T.an[:], 7, None, A.bitwise_and), ["an"], ["a8"])
        v(16, [(lambda c=c: tt(T.e1[:, 8 * c:8 * c + 8], T.fx[:, n + 8 * c:n + 8 * c + 8], T.a8[:], A.subtract)) for c in range(4)], ["fx%d" % (t + 1), "a8"], ["e1"])
        v(32, lambda: ts(T.th[:], T.e1[:], 32.0, None, A.mult), ["e1"], ["th"])

    for t in range(RO):
        gather_lists(t, 0)
        index(t, 0, 0)
        pen(t, 0, 0)
        if t == 0:
            own_mass()
            init_scalars()
        n1_chain(t)
        index(t, 0, 1)
        pen(t, 0, 1)
        if t > 0:
            thresholds(t - 1)
        gather_lists(t, 1)
        for h in range(2):
            index(t, 1, h)
            pen(t, 1, h)
        for h in range(2):
            for c in range(2):
                dld(t, c, h)
        for c, ch in [(0, 0), (0, 1), (1, 0), (1, 1), (0, 2), (1, 2), (0, 3), (1, 3)]:
            kn = score(t, c, ch)
            if c == 0:
                s(128, (lambda kn=kn, ch=ch: act(T.k0[:, 128 * ch:128 * ch + 128], T[kn][:, 0:128], F.Copy)), (), ["k0%d" % ch], [kn])
                continue
            tail(t, ch, kn)
            if t < RO - 1 and ch > 0:
                lo, hi = PARTS[ch - 1]
                o = 512 * (t + 1)
                send(t + 1, T.lw[:, o + lo:o + hi], T.rr[:, o + lo:o + hi], "al%d%d" % (t + 1, ch - 1),
                     ["rr%d_%d" % (t + 1, x) for x in range(lo // 128, hi // 128)], "lw%d_%d" % (t + 1, ch - 1))
        scalars(t)
        if t < RO - 1:
            o = 512 * (t + 1)
            send(t + 1, T.sw[:, o:o + 512], T.so[:, o:o + 512], "as%d" % (t + 1), ["so%d" % (t + 1)], "sw%d" % (t + 1))
    op("y", 0.1, [lambda: g.sync.dma_start(T.yr[:, 0:384], T.yrb[:, 0:384])], ["yrb0", "yrb1", "yrb2"], (), sem="oy", inc=16, lat=2.0)
    op("y", 0.1, [lambda: g.sync.dma_start(T.yr[:, 384:512], T.yrb[:, 384:512])], ["yrb3"], (), sem="oz", inc=16, lat=2.0)
    pe(4 * 512, [mm(T.ma[0:8, c, :], T.nx[:, 96 + 8 * c:104 + 8 * c], T.psf[:], True, True) for c in range(4)], ["nx3", "psf"], (), ["ma"])
    copy4(T.on8, 0, "on8", "ma", 8)
    op("y", 0.1, [lambda: g.sync.dma_start(T.yn[:], T.on8[:])], ["on8"], (), sem="on", inc=16, lat=2.0)
    pe(4 * 512, [mm(T.mb[0:8, c, :], T.fx[:, 96 + 8 * c:104 + 8 * c], T.psf[:], True, True) for c in range(4)], ["fx3", "psf"], (), ["mb"])
    v(128, [(lambda c=c: ts(T.of8[:, 128 * c:128 * c + 128], T.mb[0:8, c, :], -1.0, None, A.add)) for c in range(4)], (), ["of8"], ["mb"])
    op("y", 0.1, [lambda: g.sync.dma_start(T.yf[:], T.of8[:])], ["of8"], (), sem="of", inc=16, lat=2.0)
    return ops


def schedule(ops):
    n = len(ops)
    succ = [[] for _ in range(n)]
    for i, o in enumerate(ops):
        for d in o["deps"] | o["soft"]:
            succ[d].append(i)
    prio = [0.0] * n
    for i in range(n - 1, -1, -1):
        prio[i] = ops[i]["dur"] + ops[i]["lat"] + max([prio[j] for j in succ[i]], default=0.0)
    prio = [p - ALPHA * i / n for i, p in enumerate(prio)]
    left = [len(o["deps"] | o["soft"]) for o in ops]
    fin, ready, free, busy = [0.0] * n, [0.0] * n, {}, {}
    avail = [i for i in range(n) if left[i] == 0]
    order = []
    while avail:
        best = None
        for i in avail:
            q = ops[i]["q"]
            st = max(ready[i], free.get(q, 0.0)) if q else ready[i]
            k = (round(st, 3), -prio[i])
            if best is None or k < best[0]:
                best = (k, i, st)
        _, i, st = best
        avail.remove(i)
        o = ops[i]
        if o["q"]:
            free[o["q"]] = st + o["dur"]
            busy[o["q"]] = busy.get(o["q"], 0.0) + o["dur"]
        fin[i] = st + o["dur"] + o["lat"]
        order.append((st, i))
        for j in succ[i]:
            left[j] -= 1
            rt = st + o["dur"] if i in ops[j]["soft"] else fin[i] + (0.05 if ops[j]["q"] == o["q"] else 0.1)
            ready[j] = max(ready[j], rt)
            if left[j] == 0:
                avail.append(j)
    return order, fin, busy


def rank_program(g, core, T, topo):
    if T.rank_of(core) is None:
        return
    ops = build(g, T, core, topo)
    order = schedule(ops)[0]
    queue = {"v": g.vector, "s": g.scalar, "p": g.tensor, "g": g, "y": g.sync}
    own = {"v": "qv", "s": "qs", "p": "qp", "g": "qg"}
    count, known, ev, clock = {}, {}, {}, {}
    for st, i in order:
        o = ops[i]
        q = o["q"]
        if q is None:
            count[o["sem"]] = count.get(o["sem"], 0) + o["inc"]
            ev[i], clock[i] = (o["sem"], count[o["sem"]]), {}
            continue
        kn = known.setdefault(q, {})
        for d in sorted(o["deps"], reverse=True):
            sm, val = ev[d]
            if kn.get(sm, 0) < val:
                queue[q].wait_ge(T.sem[sm], val)
                kn[sm] = val
                for a, b in clock[d].items():
                    kn[a] = max(kn.get(a, 0), b)
        sm = o["sem"] or own[q]
        step = o["inc"] // len(o["fns"]) if o["sem"] else 1
        for fn in o["fns"]:
            ins = fn()
            if not o["remote"]:
                ins.then_inc(T.sem[sm], step)
            count[sm] = count.get(sm, 0) + step
        ev[i], clock[i] = (sm, count[sm]), dict(kn)
    for sm in sorted(count):
        if known.get("g", {}).get(sm, 0) < count[sm]:
            g.wait_ge(T.sem[sm], count[sm])
